import numpy as np, ml_dtypes
CORES = [6,15,38,47]
N = 4
BF = ml_dtypes.bfloat16
VX, VY, C, B, LE = 4096, 4096, 256, 4, 6
def parts(rng):
    X = rng.integers(0, 256, (N, 8, 16, VX)); Y = rng.integers(0, 256, (N, 8, 16, VY))
    K = rng.integers(0, VX, (N, 8, 16, C)); G = rng.integers(0, VY, (N, 8, 16, B * C)); W = rng.integers(0, VX, (N, 8, 16, B * C))
    z = rng.integers(0, 256, (N, 8, 16, C)); w = rng.integers(0, 64, (N, 8, 16, 1)); t = rng.integers(1000, 1451, (N, 8, 16, 1))
    return X, Y, K, G, W, z, w, t
def pack(X, Y, K, G, W, z, w, t):
    fl = lambda a: np.ascontiguousarray(np.reshape(a, (N, 128, -1))).astype(np.float32).astype(BF)
    wh = lambda a: np.ascontiguousarray(np.reshape(a, (N, 128, -1))).astype(np.int32)
    return {"gx": fl(X), "sy": fl(Y), "rk": wh(K), "rt": wh(G), "wr": wh(W), "z0": fl(z), "wt": fl(w), "th": wh(t)}
def setup_inputs(rng):
    return pack(*parts(rng))
def uneven(rng, top, bits, shape):
    v = np.exp2(bits * rng.random(shape)).astype(np.int64) - 1
    return np.minimum(np.maximum(np.where(rng.random(shape) < 0.5, v, top - v), 0), top)
def setup_inputs_spread(rng):
    X, Y, K, G, W, z, w, t = parts(rng)
    X = (np.exp2(8 * rng.random((N, 8, 1, VX))) * rng.random(X.shape)).astype(np.int64)
    Y = (np.exp2(8 * rng.random((N, 8, 1, VY))) * rng.random(Y.shape)).astype(np.int64)
    z = (np.exp2(8 * rng.random((N, 8, 1, C))) * rng.random(z.shape)).astype(np.int64)
    lx = VX.bit_length() - 1; ly = VY.bit_length() - 1
    K = uneven(rng, VX - 1, lx, K.shape); W = uneven(rng, VX - 1, lx, W.shape); G = uneven(rng, VY - 1, ly, G.shape)
    w = uneven(rng, 63, 6, w.shape); t = rng.integers(0, 4081, t.shape)
    return pack(X, Y, K, G, W, z, w, t)
def setup_inputs_ends(rng):
    sh = np.array([0.0, 0.1, 0.5, 0.9, 1.0])
    X = 255 * (rng.random((N, 8, 16, VX)) < rng.choice(sh, (N, 8, 1, VX))); Y = 255 * (rng.random((N, 8, 16, VY)) < rng.choice(sh, (N, 8, 1, VY)))
    K = (VX - 1) * rng.integers(0, 2, (N, 8, 16, C)); G = (VY - 1) * rng.integers(0, 2, (N, 8, 16, B * C)); W = (VX - 1) * rng.integers(0, 2, (N, 8, 16, B * C))
    z = 255 * rng.integers(0, 2, (N, 8, 16, C)); w = 63 * rng.integers(0, 2, (N, 8, 16, 1)); t = 4080 * (rng.random((N, 8, 16, 1)) < 0.75)
    w[:, :, 0] = 63; w[:, 0, 1] = 0; t[:, 0] = 4080; t[:, 3, :4] = 0
    for q in range(N):
        for g in range(7):
            m = (q + g) % 4
            if m == 0: X[q, g, :, 0] = 0; X[q, g, :, VX - 1] = 255
            if m == 1: X[q, g, :, 0] = 255; X[q, g, :, VX - 1] = 0
            if m == 2: X[q, g, :, 0] = 255 * rng.integers(0, 2, 16); X[q, g, :, VX - 1] = 255
            if m == 3: X[q, g, :, 0] = 255 * rng.integers(0, 2, 16); X[q, g, :, VX - 1] = 255 * rng.integers(0, 2, 16)
    m1 = [m for m in range(1, 17) if (((((255 * 63 * m) & 4095) ** 2) >> 5) & (B - 1)) == B - 1][0]
    s1 = (VY - 1 + 37 * ((255 * 63 * m1) & 4095)) & (VY - 1)
    X[:, 7, :, 0] = 0; X[:, 7, :, VX - 1] = 255; Y[:, 7, :, 0] = 0; Y[:, 7, :, VY - 1] = 255; Y[:, 7, :, s1] = 255; w[:, 7] = 63; t[:, 7] = 4080
    for i, m in ((C - 1, m1), (C - 2, 0), (C - 3, 13), (C - 4, 16), (0, m1), (1, 0), (2, 16)):
        z[:, 7, :, i] = 255 * (np.arange(16) < m)
        K[:, 7, 15, i] = 0; K[:, 7, 14, i] = VX - 1; K[:, 7, 0, i] = 0; G[:, 7, 14:, B * i:B * i + B] = VY - 1; G[:, 7, 0, B * i:B * i + B] = VY - 1
    return pack(X, Y, K, G, W, z, w, t)
def setup_inputs_corners(rng):
    X, Y, K, G, W, z, w, t = parts(rng); h = VX // 2; v = VY // 4
    X[..., :h] = rng.integers(0, 48, (N, 8, 16, h)); X[..., h:] = rng.integers(208, 256, (N, 8, 16, VX - h)); Y[..., :v] = rng.integers(0, 48, (N, 8, 16, v))
    kind = rng.integers(0, 8, (N, 8, 1, C)); kind[..., :8] = np.arange(8); kind[..., C - 8:] = np.arange(8)
    k = np.arange(16)[:, None]; lane = rng.integers(0, 16, (N, 8, 1, C))
    up = ((kind == 1) & (k == 0)) | ((kind == 2) & (k == 15)) | ((kind == 3) & (k == lane)) | ((kind == 4) & (k <= lane))
    lh = np.where(up, rng.integers(h, VX, K.shape), rng.integers(0, h, K.shape))
    K = np.where(kind == 7, (VX - 1) * rng.integers(0, 2, K.shape), np.where(kind == 6, K, lh))
    z = np.where(kind < 5, rng.integers(64, 96, z.shape), np.where(kind == 5, 255, np.where(kind == 6, 0, z)))
    M = np.zeros((8, 16), np.int64); M[1] = 4080; M[7] = 4080; M[2, 15] = 4080; M[3, 0] = 4080; M[4, ::2] = 4080; M[5, :15] = 4080
    mode = (np.arange(N)[:, None] + np.arange(8)) % 8
    t = np.where((mode == 6)[:, :, None, None], rng.choice(np.array([0, 1, 4079, 4080, 1300]), t.shape), M[mode][..., None])
    q = rng.permutation(N); t[q[0]] = 0; t[q[1]] = 4080
    a = rng.integers(0, 3, (N, 8, 1, 1)); a[:, 0] = 0; a[:, 7] = 1; w = np.where(a == 0, 0, np.where(a == 1, 63, w))
    W = np.where(rng.random((N, 8, 1, 1)) < 0.4, (VX - 1) * rng.integers(0, 2, W.shape), W)
    G = np.where(rng.random((N, 8, 1, 1)) < 0.4, (VY - 1) * rng.integers(0, 2, G.shape), G)
    z[q[1], ::2] = 0
    e = int(q[2])
    X[e] = np.minimum(X[e], 254); Y[e] = rng.integers(0, 61, Y[e].shape); K[e] = rng.integers(0, h, K[e].shape); z[e] = 255; t[e] = rng.integers(2900, 3301, t[e].shape)
    b = int(q[3]); gb = (7 - b) % 8
    X[b, gb] = np.minimum(X[b, gb], 254); z[b, gb] = 255
    return pack(X, Y, K, G, W, z, w, t)
def setup_inputs_ties(rng):
    X, Y, K, G, W, z, w, t = parts(rng)
    X[:, ::2] = 128 * rng.integers(0, 2, (N, 4, 16, VX)); Y[:, ::2] = 128 * rng.integers(0, 2, (N, 4, 16, VY))
    X[:, 1::2] = 85 * rng.integers(0, 4, (N, 4, 16, VX)); Y[:, 1::2] = 85 * rng.integers(0, 4, (N, 4, 16, VY))
    z[:, ::2] = 16 * rng.integers(0, 9, (N, 4, 16, C)); z[:, 1::2] = np.maximum(85 * rng.integers(0, 4, (N, 4, 16, C)) - 16 * rng.integers(0, 8, (N, 4, 16, C)), 0)
    t[:, ::2] = 128 * rng.integers(6, 12, (N, 4, 16, 1)); t[:, 1::2] = 85 * rng.integers(17, 24, (N, 4, 16, 1))
    t = t + rng.integers(-1, 2, t.shape) * (rng.random(t.shape) < 0.5)
    X[:, 5] = rng.integers(200, 256, (N, 16, VX)); Y[:, 5] = rng.integers(0, 61, (N, 16, VY))
    X[:, 6] = rng.integers(0, 61, (N, 16, VX)); Y[:, 6] = rng.integers(200, 256, (N, 16, VY))
    t[:, 5:7] = 3160 + rng.integers(-300, 151, (N, 2, 16, 1))
    return pack(X, Y, K, G, W, z, w, t)
def setup_inputs_alike(rng):
    X, Y, K, G, W, z, w, t = parts(rng)
    K[:, ::2] = K[:, ::2, :1, :].copy(); K[:, 1] = K[:, 1, :, :1].copy(); W[:, 1] = W[:, 1, :, :1].copy()
    W[:, 2:4] = np.repeat(K[:, 2:4], B, axis=-1); G[:, 4] = G[:, 4, :1, :1].copy(); z[:, 5] = z[:, 5, :, :1].copy()
    few = np.array([0, VX - 1, VX // 2, 3]); K[:, 7] = rng.choice(few, (N, 16, C)); W[:, 7] = rng.choice(few, (N, 16, B * C))
    return pack(X, Y, K, G, W, z, w, t)
def check_inputs(d):
    bad = []
    for k, hi in (("gx", 255), ("sy", 255), ("rk", VX - 1), ("rt", VY - 1), ("wr", VX - 1), ("z0", 255), ("wt", 63), ("th", 4080)):
        a = np.asarray(d[k]).astype(np.float64)
        if not (np.min(a) >= 0 and np.max(a) <= hi): bad.append("range of " + k)
        elif not np.all(a == np.floor(a)): bad.append("whole numbers of " + k)
    return bad
def reference(gx, sy, rk, rt, wr, z0, wt, th):
    ints = lambda a, n: a.astype(np.float32).astype(np.int32).reshape(N, 8, 16, n)
    X, Y, z, w = ints(gx, VX), ints(sy, VY), ints(z0, C), ints(wt, 1)
    K = rk.astype(np.int64).reshape(N, 8, 16, C); G = rt.astype(np.int64).reshape(N, 8, 16, B * C); W = wr.astype(np.int64).reshape(N, 8, 16, B * C)
    t = th.astype(np.int64).reshape(N, 8, 16, 1); A = np.zeros((N, 1, 1, 1), np.int64)
    margin = (16 * ((15 - np.arange(16)) >> 1)).astype(np.int32)[:, None]
    for lead in range(LE):
        if lead > 0: K = np.roll(K, 1, axis=0); z = np.roll(z, 1, axis=0)
        u = np.add.reduce(w.astype(np.int64) * z, axis=2) & 4095
        c = B * np.arange(C) + (((u * u) >> 5) & (B - 1)); cc = np.broadcast_to(c[:, :, None, :], K.shape)
        route = np.take_along_axis(G, cc, 3); old = np.take_along_axis(W, cc, 3)
        s = (((route * K) >> 5) + route + 37 * u[:, :, None, :]) & (VY - 1)
        x = np.take_along_axis(X, K.reshape(N, 8, 1, 16 * C), 3).reshape(N, 8, 16, 16, C)
        y = np.take_along_axis(Y, s.reshape(N, 8, 1, 16 * C), 3).reshape(N, 8, 16, 16, C)
        placed = np.add.reduce(np.abs(x - y), axis=2) < t + A
        hold = placed & (np.count_nonzero(x >= z[:, :, :, None, :] + margin, axis=2) >= 9)
        stop = np.logical_or.accumulate(hold[:, :, ::-1], axis=2)[:, :, ::-1]
        held = placed & stop; fail = placed & ~stop
        h, f, o = held.astype(np.int64), fail.astype(np.int64), 1 - placed.astype(np.int64)
        nh = np.add.reduce(h, axis=2)[:, :, None]; nf = np.add.reduce(f, axis=2)[:, :, None]
        over = np.add.accumulate(h[:, :, ::-1], axis=2)[:, :, ::-1] - h
        pos = np.where(held, over, np.where(fail, nh + np.add.accumulate(f, axis=2) - f, nh + nf + np.add.accumulate(o, axis=2) - o))
        new = np.zeros_like(K); np.put_along_axis(new, pos, np.where(fail, old, K), 2)
        np.put_along_axis(W, cc, np.where(fail, K, old), 3)
        z = np.abs(z - np.maximum.reduce(np.where(held[:, :, None], x, 0), axis=3))
        A = 16 * (np.add.reduce(f, axis=(1, 2, 3)) & 31).reshape(N, 1, 1, 1)
        K = new
    return {"yk": K.reshape(N, 128, C).astype(np.float32), "yw": W.reshape(N, 128, B * C).astype(np.float32), "yz": z.reshape(N, 128, C).astype(np.float32).astype(BF)}

@@ -1,0 +1,549 @@
+import numpy as np
+from concourse.bass import DstId, RemoteDMATransfer
+from concourse.mybir import dt, AluOpType, AxisListType, ActivationFunctionType
+
+A = AluOpType
+AF = ActivationFunctionType
+LE = 6
+SLOTS = ["ones", "BD0", "BD", "ID", "ID64", "NID", "IDm32", "IDh", "TGE", "SLT", "SD0", "SD", "NBD", "NSLT", "ID16",
+         "ID64t", "DE", "DX", "DK", "DKL"]
+
+SCRATCH = {
+    "X": ("sbuf", [128, 4096], "bfloat16"), "Y": ("sbuf", [128, 4096], "bfloat16"),
+    "Gf": ("sbuf", [128, 1024], "float32"), "Wf": ("sbuf", [128, 1024], "float32"),
+    "rti": ("sbuf", [128, 1024], "int32"), "wri": ("sbuf", [128, 1024], "int32"), "rki": ("sbuf", [128, 256], "int32"),
+    "thi": ("sbuf", [128, 1], "int32"), "wtb": ("sbuf", [128, 1], "bfloat16"),
+    "Z4": ("sbuf", [128, 12 * 512], "bfloat16"), "HL": ("sbuf", [128, 12 * 256], "bfloat16"),
+    "HS": ("sbuf", [128, 12 * 256], "bfloat16"), "ZS": ("sbuf", [128, 12 * 128], "bfloat16"),
+    "TB": ("sbuf", [128, 128 * len(SLOTS)], "bfloat16"),
+    "IDF": ("sbuf", [128, 128], "float32"), "ONE16": ("sbuf", [128, 128], "float32"),
+    "L1": ("sbuf", [128, 2048], "bfloat16"), "L2": ("sbuf", [128, 2048], "bfloat16"),
+    "PQ": ("sbuf", [128, 2048], "float16"), "WL": ("sbuf", [128, 2048], "bfloat16"),
+    "W37": ("sbuf", [128, 128], "float16"),
+    "COL": ("sbuf", [128, 16], "float32"), "kk": ("sbuf", [128, 16], "float32"), "RK": ("sbuf", [128, 16], "float32"),
+    "rowi": ("sbuf", [128, 2], "int32"), "r15": ("sbuf", [128, 2], "int32"),
+    "I4a": ("sbuf", [128, 8], "int32"), "I4": ("sbuf", [128, 8], "int32"),
+    "Fi": ("sbuf", [128, 1], "int32"), "Fj": ("sbuf", [128, 1], "int32"),
+    "YK": ("sbuf", [128, 256], "float32"), "hI": ("sbuf", [128, 256], "int32"), "lI": ("sbuf", [128, 256], "int32"),
+}
+for _c in range(2):
+    for _n, _w, _d in (("K16", 128, "uint16"), ("x", 2048, "bfloat16"), ("d", 2048, "bfloat16"), ("sg", 2048, "bfloat16"),
+                       ("ua", 8, "int32"), ("ub", 8, "int32"), ("uc", 8, "int32"), ("ud", 8, "int32"), ("ue", 8, "int32"),
+                       ("c16", 8, "uint16"), ("Gs", 128, "float32"), ("Wo", 128, "float32"), ("dk", 128, "float32"),
+                       ("dl", 128, "float32"), ("val", 128, "float32"), ("p1", 128, "int32"), ("pr", 128, "int32"),
+                       ("s1", 128, "int32"), ("s2", 128, "int32"), ("s16", 128, "uint16"), ("o", 128, "bfloat16"),
+                       ("hd", 128, "bfloat16"), ("eo", 128, "bfloat16"), ("f", 128, "bfloat16"), ("h", 128, "bfloat16"),
+                       ("m", 128, "bfloat16"), ("h64", 128, "bfloat16"), ("WW", 256, "float16"),
+                       ("CL", 15 * 256, "float16"), ("AC", 256, "float16"), ("mz", 128, "float16"), ("Fs", 1, "float32")):
+        SCRATCH[_n + str(_c)] = ("sbuf", [128, _w], _d)
+for _b in range(8):
+    SCRATCH["ps%d" % _b] = ("psum", [128, 512], "float32")
+
+SEMAPHORES = ["eV", "eS", "eT", "eG", "loc"] + ["ld%d" % _i for _i in range(20)] + ["st%d" % _i for _i in range(8)]
+for _e in range(LE):
+    for _c in range(2):
+        SEMAPHORES += ["zr%d_%d" % (_e, _c), "ah%d_%d" % (_e, _c), "az%d_%d" % (_e, _c)]
+
+CY = 0.83e-3 * 1.25
+TC = 0.42e-3 * 1.25
+GAT = 1.55
+SCA = 3.8
+HOP = 0.06
+
+
+def rank_program(g, core, T, topo):
+    rank = T.rank_of(core)
+    if rank is None:
+        return
+    cores = list(T.cores)
+    dst = cores[(rank + 1) % len(cores)]
+    rid, pid, _s = topo.addr(dst)
+    engines = topo.engines(core, dst)
+    emask = topo.mask(core, dst)
+    neng = len(engines)
+
+    V, S, TE, SY = g.vector, g.scalar, g.tensor, g.sync
+    QS = {"V": V, "S": S, "T": TE, "G": g, "Y": SY}
+    ops, acc = [], {}
+
+    def add(q, dur, emit, R=(), W=(), kind="c", sem=None, val=0, lat=0.0, extra=()):
+        i = len(ops)
+        deps = {}
+        for j in extra:
+            deps[j] = False
+        for isw, regs in ((False, R), (True, W)):
+            for buf, lo, hi in regs:
+                lst = acc.setdefault(buf, [])
+                ps = buf[:2] == "ps"
+                keep = []
+                for a in lst:
+                    j, l, h, aw = a
+                    if j == i:
+                        keep.append(a)
+                        continue
+                    over = ps or (l < hi and lo < h)
+                    same = ops[j]["q"] == q and ops[j]["kind"] == "c" and kind == "c"
+                    if over:
+                        if ps:
+                            deps[j] = deps.get(j, False) or not same
+                        elif isw or aw:
+                            deps[j] = deps.get(j, False) or (aw if same else True)
+                    if ps and same:
+                        continue
+                    if isw and (not ps) and l >= lo and h <= hi:
+                        continue
+                    keep.append(a)
+                keep.append((i, lo, hi, isw))
+                acc[buf] = keep
+        ops.append({"q": q, "dur": dur, "emit": emit, "deps": deps, "kind": kind, "sem": sem, "val": val, "lat": lat})
+        return i
+
+    def vt(n, rate=1.0):
+        return 0.03 + max(64, n * rate) * CY
+
+    def tt(n, cnt=1, f=1):
+        return 0.02 + cnt * max(64, n) * TC * f
+
+    def sl(n):
+        s = SLOTS.index(n)
+        return T.TB[:, 128 * s:128 * s + 128]
+
+    def rs(n):
+        s = SLOTS.index(n)
+        return ("TB", 128 * s, 128 * s + 128)
+
+    def col(i):
+        return T.COL[:, i:i + 1]
+
+    def rc(i):
+        return ("COL", i, i + 1)
+
+    def mm(o, l, r, a, b):
+        return TE.matmul(o, l, r, a, b)
+
+    def ts(out, in0, s1, s2, op0, op1=None):
+        if op1 is None:
+            return V.tensor_scalar(out, in0, s1, None, op0)
+        return V.tensor_scalar(out, in0, s1, s2, op0, op1)
+
+    nld = [0]
+
+    def load(q, out, in_, reg, dur, lat):
+        s = "ld%d" % nld[0]
+        nld[0] += 1
+        eng = QS[q]
+        add(q, dur, lambda: eng.dma_start(out, in_), (), (reg,), kind="d", sem=s, val=16, lat=lat)
+
+    load("Y", T.rki[:, :], T.rk[:, :], ("rki", 0, 256), 0.1, 2.2)
+    load("S", T.Z4[:, 0:128], T.z0[:, 0:128], ("Z4", 0, 128), 0.1, 2.2)
+    load("S", T.wtb[:, :], T.wt[:, :], ("wtb", 0, 1), 0.1, 2.2)
+    load("Y", T.rti[:, 0:512], T.rt[:, 0:512], ("rti", 0, 512), 0.1, 3.5)
+    load("S", T.X[:, :], T.gx[:, :], ("X", 0, 4096), 0.1, 6.5)
+    load("S", T.Z4[:, 512:640], T.z0[:, 128:256], ("Z4", 512, 640), 0.1, 6.5)
+    load("Y", T.Y[:, :], T.sy[:, :], ("Y", 0, 4096), 0.1, 9.5)
+    load("Y", T.thi[:, :], T.th[:, :], ("thi", 0, 1), 0.1, 9.5)
+    load("Y", T.wri[:, 0:512], T.wr[:, 0:512], ("wri", 0, 512), 0.1, 10.5)
+    load("Y", T.rti[:, 512:1024], T.rt[:, 512:1024], ("rti", 512, 1024), 0.1, 11.5)
+    load("Y", T.wri[:, 512:1024], T.wr[:, 512:1024], ("wri", 512, 1024), 0.1, 12.5)
+
+    add("V", vt(128, .5), lambda: V.memset(sl("ones"), 1.0), (), (rs("ones"),))
+    add("G", .4, lambda: g.iota(T.rowi[:, 0:1], [[0, 1]], 0, 1), (), (("rowi", 0, 1),))
+    add("G", .4, lambda: g.affine_select(sl("BD0"), sl("ones"), [[-16, 8], [0, 16]], A.is_ge, 0.0, 0, 1), (rs("ones"),), (rs("BD0"),))
+    add("G", .4, lambda: g.affine_select(sl("BD"), sl("BD0"), [[16, 8], [0, 16]], A.is_ge, 0.0, 15, -1), (rs("BD0"),), (rs("BD"),))
+    add("G", .4, lambda: g.affine_select(sl("ID"), sl("ones"), [[-1, 128]], A.is_equal, 0.0, 0, 1), (rs("ones"),), (rs("ID"),))
+    add("G", .2, lambda: g.iota(T.I4a[:, :], [[64, 8]], 0, 0), (), (("I4a", 0, 8),))
+    add("G", .2, lambda: g.iota(T.kk[:, :], [[1, 16]], 0, 0, allow_small_or_imprecise_dtypes=True), (), (("kk", 0, 16),))
+    add("G", .4, lambda: g.affine_select(sl("TGE"), sl("BD"), [[-1, 128]], A.is_ge, 0.0, 0, 1), (rs("BD"),), (rs("TGE"),))
+    add("V", vt(1), lambda: ts(T.r15[:, 0:1], T.rowi[:, 0:1], 15, None, A.bitwise_and), (("rowi", 0, 1),), (("r15", 0, 1),))
+    add("V", vt(1), lambda: V.tensor_copy(col(0), T.r15[:, 0:1]), (("r15", 0, 1),), (rc(0),))
+
+    def lin(o, i, a, b):
+        add("V", vt(1), lambda: ts(col(o), col(i), float(a), float(b), A.mult, A.add), (rc(i),), (rc(o),))
+    lin(10, 0, 4, 0)
+    add("V", vt(8), lambda: ts(T.I4[:, :], T.I4a[:, :], col(10), None, A.add), (("I4a", 0, 8), rc(10)), (("I4", 0, 8),))
+
+    def scl(o, i, a):
+        add("V", vt(128, .5), lambda: ts(sl(o), sl(i), float(a), None, A.mult), (rs(i),), (rs(o),))
+    scl("ID64", "ID", 64)
+    add("V", vt(2048, .5), lambda: V.memset(T.L1[:, :], 0.0), (), (("L1", 0, 2048),))
+
+    def cpy(buf, base, off, src):
+        add("V", vt(8), lambda: V.tensor_copy(T[buf][:, base + off:base + 128:16], T.TB[:, 128 * SLOTS.index(src) + off:128 * SLOTS.index(src) + 128:16]), (rs(src),), ((buf, base + off, base + off + 113),))
+    for k in range(16):
+        cpy("L1", 128 * k, k, "BD")
+    add("V", vt(2048, .5), lambda: ts(T.WL[:, :], T.L1[:, :], T.wtb[:, 0:1], None, A.mult), (("L1", 0, 2048), ("wtb", 0, 1)), (("WL", 0, 2048),))
+    add("V", vt(1), lambda: ts(col(7), T.wtb[:, 0:1], 37.0, None, A.mult), (("wtb", 0, 1),), (rc(7),))
+    add("V", vt(1), lambda: ts(col(8), col(7), 2048.0, -4096.0, A.is_gt, A.mult), (rc(7),), (rc(8),))
+    add("V", vt(1), lambda: V.tensor_tensor(col(9), col(7), col(8), A.add), (rc(7), rc(8)), (rc(9),))
+    add("V", vt(128, .5), lambda: ts(T.W37[:, :], sl("BD"), col(9), None, A.mult), (rs("BD"), rc(9)), (("W37", 0, 128),))
+    add("V", vt(128), lambda: V.tensor_copy(T.IDF[:, :], sl("ID")), (rs("ID"),), (("IDF", 0, 128),))
+
+    def hl0(c):
+        a, b = 128 * c, 128 * c + 128
+        add("V", vt(128), lambda: ts(T.hI[:, a:b], T.rki[:, a:b], 6, None, A.arith_shift_right), (("rki", 0, 256),), (("hI", a, b),))
+        add("V", vt(128), lambda: ts(T.lI[:, a:b], T.rki[:, a:b], 63, None, A.bitwise_and), (("rki", 0, 256),), (("lI", a, b),))
+        add("V", vt(128), lambda: V.tensor_copy(T.HL[:, 256 * c:256 * c + 128], T.hI[:, a:b]), (("hI", a, b),), (("HL", 256 * c, 256 * c + 128),))
+        add("V", vt(128), lambda: V.tensor_copy(T.HL[:, 256 * c + 128:256 * c + 256], T.lI[:, a:b]), (("lI", a, b),), (("HL", 256 * c + 128, 256 * c + 256),))
+    hl0(0)
+    hl0(1)
+
+    def conv(dst_, src, c):
+        a, b = 512 * c, 512 * c + 512
+        add("V", vt(512), lambda: V.tensor_copy(T[dst_][:, a:b], T[src][:, a:b]), ((src, a, b),), ((dst_, a, b),))
+    conv("Gf", "rti", 0)
+    conv("Wf", "wri", 0)
+    conv("Gf", "rti", 1)
+    conv("Wf", "wri", 1)
+    add("V", vt(1), lambda: V.tensor_copy(col(11), T.thi[:, 0:1]), (("thi", 0, 1),), (rc(11),))
+    lin(1, 0, -1, 15)
+    lin(2, 0, -2, 15)
+    lin(3, 0, 64, 0)
+    lin(4, 0, 64, 8256)
+    lin(5, 0, 64, -960)
+    scl("NID", "ID", -1)
+    scl("IDm32", "ID", -1 / 32)
+    scl("IDh", "ID", 0.5)
+    scl("ID16", "ID", 1 / 16)
+    scl("ID64t", "ID", 1 / 64)
+    scl("NBD", "BD", -1)
+    add("V", vt(128, 2), lambda: V.tensor_tensor(sl("SLT"), sl("BD"), sl("TGE"), A.subtract), (rs("BD"), rs("TGE")), (rs("SLT"),))
+    add("V", vt(128, 2), lambda: V.tensor_tensor(sl("SD0"), sl("SLT"), sl("TGE"), A.subtract), (rs("SLT"), rs("TGE")), (rs("SD0"),))
+    add("V", vt(128, 2), lambda: V.tensor_tensor(sl("SD0"), sl("SD0"), sl("ID"), A.add), (rs("SD0"), rs("ID")), (rs("SD0"),))
+    scl("SD", "SD0", 1 / 1024)
+    scl("NSLT", "SLT", -1 / 16)
+    for nm, ci in (("DE", 1), ("DX", 2), ("DK", 3), ("DKL", 4)):
+        def dg(nm=nm, ci=ci):
+            add("V", vt(128, .5), lambda: ts(sl(nm), sl("ID"), col(ci), None, A.mult), (rs("ID"), rc(ci)), (rs(nm),))
+        dg()
+    add("V", vt(128), lambda: V.memset(T.ONE16[:, :], 16.0), (), (("ONE16", 0, 128),))
+    add("V", vt(16), lambda: ts(T.RK[:, :], T.kk[:, :], col(0), None, A.is_equal), (("kk", 0, 16), rc(0)), (("RK", 0, 16),))
+    for k in range(16):
+        def l2(k=k):
+            add("V", vt(128, .5), lambda: ts(T.L2[:, 128 * k:128 * k + 128], sl("BD"), T.RK[:, k:k + 1], 256.0, A.mult, A.mult),
+                (rs("BD"), ("RK", 0, 16)), (("L2", 128 * k, 128 * k + 128),))
+        l2()
+    add("V", vt(2048, .5), lambda: V.tensor_scalar(T.CL0[:, 0:2048], T.L1[:, :], 0.0, None, A.mult), (("L1", 0, 2048),), (("CL0", 0, 2048),))
+    add("V", vt(2048, .5), lambda: V.tensor_copy(T.PQ[:, :], T.CL0[:, 0:2048]), (("CL0", 0, 2048),), (("PQ", 0, 2048),))
+    for k in range(16):
+        cpy("PQ", 128 * k, k, "BD")
+        if k < 15:
+            cpy("PQ", 128 * k, k + 1, "NBD")
+
+    for e in range(LE):
+        for c in range(2):
+            _lead(e, c, T, g, V, S, TE, SY, add, vt, tt, sl, rs, col, rc, mm, ts, rid, pid, emask, neng, ops)
+
+    n = len(ops)
+    succ = [[] for _ in range(n)]
+    cnt = [0] * n
+    for i, o in enumerate(ops):
+        for j in o["deps"]:
+            succ[j].append(i)
+        cnt[i] = len(o["deps"])
+    tail = [0.0] * n
+    for i in range(n - 1, -1, -1):
+        o = ops[i]
+        tail[i] = o["dur"] + o["lat"] + max([tail[k] + HOP for k in succ[i]] + [0.0])
+    free = {}
+    ready = [0.0] * n
+    cand = {}
+    for i in range(n):
+        if cnt[i] == 0:
+            cand.setdefault(ops[i]["q"], []).append(i)
+    order = []
+    while True:
+        best = None
+        for q, lst in cand.items():
+            if not lst:
+                continue
+            fq = free.get(q, 0.0)
+            st = min(max(fq, ready[i]) for i in lst)
+            pick = max((i for i in lst if max(fq, ready[i]) <= st + 0.02), key=lambda i: (tail[i], -i))
+            if best is None or st < best[0]:
+                best = (st, q, pick)
+        if best is None:
+            break
+        _st, q, i = best
+        cand[q].remove(i)
+        start = max(free.get(q, 0.0), ready[i])
+        if ops[i]["kind"] == "r":
+            end = start
+        else:
+            end = start + ops[i]["dur"]
+            free[q] = end
+        end += ops[i]["lat"]
+        order.append(i)
+        for k in succ[i]:
+            ready[k] = max(ready[k], end + HOP)
+            cnt[k] -= 1
+            if cnt[k] == 0:
+                cand.setdefault(ops[k]["q"], []).append(k)
+    if len(order) != n:
+        raise ValueError("cycle")
+
+    count = {"V": 0, "S": 0, "T": 0, "G": 0}
+    known = {q: {} for q in ("V", "S", "T", "G", "Y")}
+    nsend = 0
+    for i in order:
+        o = ops[i]
+        q = o["q"]
+        if o["kind"] == "r":
+            o["clk"] = {o["sem"]: o["val"]}
+            continue
+        kn = known[q]
+        for j in sorted((j for j, w in o["deps"].items() if w), key=lambda j: -order.index(j) if False else -j):
+            p = ops[j]
+            if p["kind"] == "s":
+                raise ValueError("nothing waits for a send")
+            sem, val = (p["sem"], p["val"]) if p["kind"] != "c" else ("e" + p["q"], p["pos"])
+            if kn.get(sem, 0) < val:
+                QS[q].wait_ge(T.sem[sem], val)
+                for s2, v2 in p["clk"].items():
+                    if kn.get(s2, 0) < v2:
+                        kn[s2] = v2
+        ins = o["emit"]()
+        clk = dict(kn)
+        if o["kind"] == "c":
+            count[q] += 1
+            o["pos"] = count[q]
+            ins.then_inc(T.sem["e" + q], 1)
+            clk["e" + q] = count[q]
+        elif o["kind"] == "d":
+            if ins is not None:
+                ins.then_inc(T.sem[o["sem"]], 16)
+            clk[o["sem"]] = o["val"]
+        else:
+            nsend += 1
+        o["clk"] = clk
+    kn = known["Y"]
+    for q in ("V", "S", "T", "G"):
+        SY.wait_ge(T.sem["e" + q], count[q])
+    for o in ops:
+        if o["kind"] in ("d", "r"):
+            if kn.get(o["sem"], 0) < o["val"]:
+                SY.wait_ge(T.sem[o["sem"]], o["val"])
+                kn[o["sem"]] = o["val"]
+    g.wait_ge(T.sem.loc, neng * nsend)
+
+
+def _lead(e, c, T, g, V, S, TE, SY, add, vt, tt, sl, rs, col, rc, mm, ts, rid, pid, emask, neng, ops):
+    first, last = e == 0, e == LE - 1
+    n = 2 * e + c
+    B = lambda nm: T[nm + str(c)]
+    R = lambda nm, a=0, b=None: (nm + str(c), a, b if b is not None else SCRATCH[nm + str(c)][1][1])
+    P = lambda b: T["ps%d" % b]
+    PR = lambda b: ("ps%d" % b, 0, 512)
+    zb, hb = 512 * n, 256 * n
+    z = T.Z4[:, zb:zb + 128]
+    hi, lo = T.HL[:, hb:hb + 128], T.HL[:, hb + 128:hb + 256]
+    rz, rhl = ("Z4", zb, zb + 128), ("HL", hb, hb + 256)
+    if not first:
+        sh, sz = _lead_sends[(e - 1, c)]
+        add("R", 0, None, (), (rhl,), kind="r", sem="ah%d_%d" % (e, c), val=neng, lat=3.0, extra=(sh,))
+        add("R", 0, None, (), (rz,), kind="r", sem="az%d_%d" % (e, c), val=neng, lat=3.0, extra=(sz,))
+
+    def zrep():
+        s = T.sem["zr%d_%d" % (e, c)]
+        for j in range(1, 4):
+            SY.dma_start(T.Z4[:, zb + 128 * j:zb + 128 * j + 128], z).then_inc(s, 16)
+        return None
+    add("Y", 0.3, zrep, (rz,), (("Z4", zb + 128, zb + 512),), kind="d", sem="zr%d_%d" % (e, c), val=48, lat=2.2)
+
+    def fK(o):
+        mm(o, sl("ID64"), hi, True, False)
+        return mm(o, sl("ID"), lo, False, True)
+    Kp = P(7)[:, 0:128]
+    add("T", tt(128, 2), lambda: fK(Kp), (rhl, rs("ID64"), rs("ID")), (PR(7),))
+    add("V", vt(128), lambda: V.tensor_copy(B("K16")[:, :], Kp), (PR(7),), (R("K16"),))
+
+    def fU():
+        for r in range(16):
+            i = mm(P(7)[:, 128:136], T.WL[:, 128 * r:128 * r + 128], T.Z4[:, zb + r:zb + 128:16], r == 0, r == 15)
+        return i
+    add("T", tt(8, 16), fU, (rz, ("WL", 0, 2048)), (PR(7),))
+    add("V", vt(8), lambda: V.tensor_copy(B("ua")[:, :], P(7)[:, 128:136]), (PR(7),), (R("ua"),))
+    add("V", vt(8), lambda: ts(B("ub")[:, :], B("ua")[:, :], 63, None, A.bitwise_and), (R("ua"),), (R("ub"),))
+    add("V", vt(8), lambda: V.tensor_tensor(B("uc")[:, :], B("ub")[:, :], B("ub")[:, :], A.mult), (R("ub"),), (R("uc"),))
+    add("V", vt(8), lambda: ts(B("ud")[:, :], B("uc")[:, :], 5, 3, A.arith_shift_right, A.bitwise_and), (R("uc"),), (R("ud"),))
+    add("V", vt(8), lambda: V.tensor_tensor(B("ue")[:, :], B("ud")[:, :], T.I4[:, :], A.add), (R("ud"), ("I4", 0, 8)), (R("ue"),))
+    add("V", vt(8), lambda: V.tensor_copy(B("c16")[:, :], B("ue")[:, :]), (R("ue"),), (R("c16"),))
+    wa, wb = 512 * c, 512 * c + 512
+    add("S", vt(128, GAT), lambda: S.activation(B("Gs")[:, :], T.Gf[:, wa:wb].indirect(B("c16")[:, 0:8]), AF.Copy),
+        (R("c16"), ("Gf", wa, wb)), (R("Gs"),))
+    add("V", vt(128), lambda: V.tensor_tensor(B("p1")[:, :], B("Gs")[:, :], Kp, A.mult), (R("Gs"), PR(7)), (R("p1"),))
+
+    def fv():
+        mm(P(7)[:, 256:384], T.W37[:, :], z, True, False)
+        return mm(P(7)[:, 256:384], T.IDF[:, :], B("Gs")[:, :], False, True)
+    add("T", tt(128, 5), fv, (rz, ("W37", 0, 128), ("IDF", 0, 128), R("Gs")), (PR(7),))
+    add("V", vt(128), lambda: ts(B("pr")[:, :], B("p1")[:, :], 5, None, A.arith_shift_right), (R("p1"),), (R("pr"),))
+    add("V", vt(128), lambda: V.tensor_tensor(B("s1")[:, :], B("pr")[:, :], P(7)[:, 256:384], A.add), (R("pr"), PR(7)), (R("s1"),))
+    add("V", vt(128), lambda: ts(B("s2")[:, :], B("s1")[:, :], 4095, None, A.bitwise_and), (R("s1"),), (R("s2"),))
+    add("V", vt(128), lambda: V.tensor_copy(B("s16")[:, :], B("s2")[:, :]), (R("s2"),), (R("s16"),))
+    for hf in range(2):
+        def fx(hf=hf):
+            return S.activation(B("x")[:, 1024 * hf:1024 * hf + 1024], T.X[:, :].indirect(B("K16")[:, 64 * hf:64 * hf + 64]), AF.Copy)
+        add("S", vt(1024, GAT), fx, (R("K16"), ("X", 0, 4096)), (R("x", 1024 * hf, 1024 * hf + 1024),))
+    add("S", vt(128, GAT), lambda: S.activation(B("Wo")[:, :], T.Wf[:, wa:wb].indirect(B("c16")[:, 0:8]), AF.Copy),
+        (R("c16"), ("Wf", wa, wb)), (R("Wo"),))
+    add("V", vt(128), lambda: V.tensor_tensor(B("dk")[:, :], B("Wo")[:, :], Kp, A.subtract), (R("Wo"), PR(7)), (R("dk"),))
+    for hf in range(2):
+        a, b = 1024 * hf, 1024 * hf + 1024
+
+        def fy(hf=hf, a=a, b=b):
+            return V.tensor_tensor(B("d")[:, a:b], T.Y[:, :].indirect(B("s16")[:, 64 * hf:64 * hf + 64]), B("x")[:, a:b], A.subtract)
+        add("V", vt(1024, GAT), fy, (R("s16"), ("Y", 0, 4096), R("x", a, b)), (R("d", a, b),))
+
+        def fa(a=a, b=b):
+            return S.activation(B("d")[:, a:b], B("d")[:, a:b], AF.Abs)
+        add("S", vt(1024), fa, (R("d", a, b),), (R("d", a, b),))
+
+        def fD(hf=hf, a=a, b=b):
+            for k in range(16):
+                i = mm(P(4)[:, 64 * hf:64 * hf + 64], T.L1[:, 128 * k:128 * k + 128], B("d")[:, a + k:b:16], k == 0, k == 15)
+            return i
+        add("T", tt(64, 16), fD, (R("d", a, b), ("L1", 0, 2048)), (PR(4),))
+    for bk in range(4):
+        def fb(bk=bk):
+            mm(P(bk)[:, 0:512], sl("NID"), T.Z4[:, zb:zb + 512], True, False)
+            for j in range(4):
+                i = mm(P(bk)[:, 128 * j:128 * j + 128], sl("ID"), B("x")[:, 4 * bk + j:2048:16], False, j == 3)
+            return i
+        add("T", tt(512, 2), fb, (("Z4", zb, zb + 512), R("x"), rs("ID"), rs("NID")), (PR(bk),))
+        for j in range(2):
+            pr = 2 * bk + j
+
+            def fs(bk=bk, j=j, pr=pr):
+                return S.activation(B("sg")[:, 256 * pr:256 * pr + 256], P(bk)[:, 256 * j:256 * j + 256], AF.Sign, bias=0.5 - 16.0 * (7 - pr))
+            add("S", vt(256), fs, (PR(bk),), (R("sg", 256 * pr, 256 * pr + 256),))
+    for bk in range(4):
+        def fc(bk=bk):
+            for j in range(4):
+                k = 4 * bk + j
+                i = mm(P(5)[:, 0:128], T.L1[:, 128 * k:128 * k + 128], B("sg")[:, 128 * k:128 * k + 128], k == 0, False)
+            return i
+        add("T", tt(128, 4), fc, (R("sg", 512 * bk, 512 * bk + 512), ("L1", 0, 2048)), (PR(5),))
+    thr = 11 if first else 12
+    o, f, h = B("o")[:, :], B("f")[:, :], B("h")[:, :]
+    add("V", vt(128), lambda: ts(o, P(4)[:, 0:128], col(thr), 1024.0, A.is_ge, A.mult), (PR(4), rc(thr)), (R("o"),))
+    add("T", tt(128), lambda: mm(P(5)[:, 0:128], sl("IDm32"), o, False, True), (R("o"), rs("IDm32")), (PR(5),))
+    add("S", vt(128), lambda: S.activation(B("hd")[:, :], P(5)[:, 0:128], AF.Relu), (PR(5),), (R("hd"),))
+
+    def fE():
+        mm(P(4)[:, 128:256], sl("DE"), sl("ones"), True, False)
+        return mm(P(4)[:, 128:256], sl("SD"), o, False, True)
+    add("T", tt(128, 2), fE, (R("o"), rs("DE"), rs("SD"), rs("ones")), (PR(4),))
+    add("V", vt(128), lambda: V.tensor_tensor(B("eo")[:, :], o, P(4)[:, 128:256], A.mult), (R("o"), PR(4)), (R("eo"),))
+
+    def fF():
+        mm(P(5)[:, 128:256], sl("TGE"), B("hd")[:, :], True, False)
+        return mm(P(5)[:, 128:256], sl("IDh"), o, False, True)
+    add("T", tt(128, 2), fF, (R("o"), R("hd"), rs("TGE"), rs("IDh")), (PR(5),))
+    add("S", vt(128), lambda: S.activation(f, P(5)[:, 128:256], AF.Relu, bias=1.0, scale=-1.0, accum_out=B("Fs")[:, 0:1]),
+        (PR(5),), (R("f"), R("Fs")))
+    add("V", vt(128), lambda: V.tensor_tensor(h, P(5)[:, 128:256], o, A.is_gt), (PR(5), R("o")), (R("h"),))
+
+    def fX():
+        mm(P(4)[:, 384:512], sl("ID"), f, True, True)
+        mm(P(4)[:, 256:384], sl("DX"), sl("ones"), True, False)
+        mm(P(4)[:, 256:384], sl("SD"), o, False, False)
+        return mm(P(4)[:, 256:384], sl("NBD"), f, False, True)
+    add("T", tt(128, 4), fX, (R("o"), R("f"), rs("DX"), rs("SD"), rs("NBD"), rs("ones"), rs("ID")), (PR(4),))
+
+    def fK2():
+        return fK(P(6)[:, 256:384])
+    add("T", tt(128, 2), fK2, (rhl, rs("ID64"), rs("ID")), (PR(6),))
+    add("V", vt(128), lambda: V.tensor_tensor(B("dl")[:, :], B("dk")[:, :], P(4)[:, 384:512], A.mult), (R("dk"), PR(4)), (R("dl"),))
+    add("V", vt(128), lambda: V.tensor_tensor(B("val")[:, :], B("dl")[:, :], P(6)[:, 256:384], A.add), (R("dl"), PR(6)), (R("val"),))
+    add("S", vt(128), lambda: S.activation(B("h64")[:, :], B("val")[:, :], AF.Copy, bias=8224.5), (R("val"),), (R("h64"),))
+    add("V", vt(128), lambda: V.tensor_tensor(B("m")[:, :], h, P(4)[:, 256:384], A.mult), (R("h"), PR(4)), (R("m"),))
+
+    def fW(o_, dk, hs):
+        mm(o_, sl(dk), sl("ones"), True, False)
+        mm(o_, sl("NSLT"), o, False, False)
+        mm(o_, sl("ID16"), B("eo")[:, :], False, False)
+        return mm(o_, sl("ID64"), B("m")[:, :], False, False)
+    wr_ = (R("o"), R("eo"), R("m"), rs("ones"), rs("NSLT"), rs("ID16"), rs("ID64"), rs("DK"), rs("DKL"))
+    add("T", tt(128, 4), lambda: fW(P(5)[:, 256:384], "DK", None), wr_, (PR(5),))
+    add("T", tt(128, 4), lambda: fW(P(4)[:, 0:128], "DKL", None), wr_, (PR(4),))
+    add("T", tt(128), lambda: mm(P(5)[:, 256:384], sl("ID64t"), B("h64")[:, :], False, True), (R("h64"), rs("ID64t")), (PR(5),))
+    add("T", tt(128), lambda: mm(P(4)[:, 0:128], sl("NID"), B("h64")[:, :], False, True), (R("h64"), rs("NID")), (PR(4),))
+    add("V", vt(128), lambda: ts(B("WW")[:, 0:128], P(5)[:, 256:384], -129.0, None, A.add), (PR(5),), (R("WW", 0, 128),))
+    add("V", vt(128), lambda: V.tensor_tensor(B("WW")[:, 128:256], B("val")[:, :], P(4)[:, 0:128], A.add), (R("val"), PR(4)), (R("WW", 128, 256),))
+    if c == 1 and not last:
+        def fF2():
+            mm(P(6)[:, 384:385], T.ONE16[:, :], T.Fs0[:, 0:1], True, False)
+            return mm(P(6)[:, 384:385], T.ONE16[:, :], T.Fs1[:, 0:1], False, True)
+        add("T", tt(64, 8), fF2, (("Fs0", 0, 1), ("Fs1", 0, 1), ("ONE16", 0, 128)), (PR(6),))
+        add("V", vt(1), lambda: V.tensor_copy(T.Fi[:, 0:1], P(6)[:, 384:385]), (PR(6),), (("Fi", 0, 1),))
+        add("V", vt(1), lambda: ts(T.Fj[:, 0:1], T.Fi[:, 0:1], 511, None, A.bitwise_and), (("Fi", 0, 1),), (("Fj", 0, 1),))
+        add("V", vt(1), lambda: V.tensor_tensor(col(12), T.Fj[:, 0:1], col(11), A.add), (("Fj", 0, 1), rc(11)), (rc(12),))
+    for q in range(15):
+        def fq(q=q):
+            return ts(B("CL")[:, 256 * q:256 * q + 256], B("WW")[:, :], 64.0 * (q + 1), None, A.min)
+        add("V", vt(256, .5), fq, (R("WW"),), (R("CL", 256 * q, 256 * q + 256),))
+    add("T", tt(256), lambda: mm(P(6)[:, 0:256], T.PQ[:, 1920:2048], B("WW")[:, :], True, False), (R("WW"), ("PQ", 0, 2048)), (PR(6),))
+    for q0 in range(0, 15, 3):
+        def fp(q0=q0):
+            for q in range(q0, q0 + 3):
+                i = mm(P(6)[:, 0:256], T.PQ[:, 128 * q:128 * q + 128], B("CL")[:, 256 * q:256 * q + 256], False, q == 14)
+            return i
+        add("T", tt(256, 3), fp, (R("CL", 256 * q0, 256 * q0 + 768), ("PQ", 0, 2048)), (PR(6),))
+    add("S", vt(256), lambda: S.activation(T.HS[:, hb:hb + 256], P(6)[:, 0:256], AF.Identity, bias=col(5)), (PR(6), rc(5)), (("HS", hb, hb + 256),))
+    sh = None
+    if not last:
+        nb = 256 * (n + 2)
+
+        def sendh():
+            return g.remote_dma(out_ap=T.HL[:, nb:nb + 256], in_ap=T.HS[:, hb:hb + 256], remote_sem=T.sem["ah%d_%d" % (e + 1, c)],
+                                local_sem=T.sem.loc, pid=pid, routing_id=rid, dma_engine_mask=emask)
+        sh = add("G", 1.0, sendh, (("HS", hb, hb + 256),), (), kind="s")
+    else:
+        def fK3():
+            mm(P(7)[:, 0:128], sl("ID64"), T.HS[:, hb:hb + 128], True, False)
+            return mm(P(7)[:, 0:128], sl("ID"), T.HS[:, hb + 128:hb + 256], False, True)
+        add("T", tt(128, 2), fK3, (("HS", hb, hb + 256), rs("ID64"), rs("ID")), (PR(7),))
+        add("S", vt(128), lambda: S.activation(T.YK[:, 128 * c:128 * c + 128], P(7)[:, 0:128], AF.Copy), (PR(7),), (("YK", 128 * c, 128 * c + 128),))
+        add("Y", .1, lambda: SY.dma_start(T.yk[:, 128 * c:128 * c + 128], T.YK[:, 128 * c:128 * c + 128]), (("YK", 128 * c, 128 * c + 128),), (),
+            kind="d", sem="st%d" % c, val=16, lat=2.2)
+    add("V", vt(128, SCA), lambda: V.tensor_tensor(T.Wf[:, wa:wb].indirect(B("c16")[:, 0:8]), B("Wo")[:, :], B("dl")[:, :], A.subtract),
+        (R("Wo"), R("dl"), R("c16")), (("Wf", wa, wb),))
+    if last:
+        add("Y", .1, lambda: SY.dma_start(T.yw[:, wa:wb], T.Wf[:, wa:wb]), (("Wf", wa, wb),), (), kind="d", sem="st%d" % (2 + c), val=16, lat=2.5)
+    for bk in range(4):
+        def fm(bk=bk):
+            for j in range(4):
+                k = 4 * bk + j
+                mm(P(bk)[:, 128 * j:128 * j + 128], sl("ID"), B("x")[:, k:2048:16], True, False)
+                i = mm(P(bk)[:, 128 * j:128 * j + 128], T.L2[:, 128 * k:128 * k + 128], h, False, True)
+            return i
+        add("T", tt(128, 8), fm, (R("h"), R("x"), ("L2", 0, 2048), rs("ID")), (PR(bk),))
+        for j in range(2):
+            def fM(bk=bk, j=j):
+                src = P(bk)[:, 256 * j:256 * j + 256]
+                if bk == 0 and j == 0:
+                    return ts(B("AC")[:, :], src, 256.0, None, A.max)
+                return V.tensor_tensor(B("AC")[:, :], B("AC")[:, :], src, A.max)
+            add("V", vt(256), fM, (PR(bk),) if bk == 0 and j == 0 else (R("AC"), PR(bk)), (R("AC"),))
+    add("V", vt(128, 2), lambda: V.tensor_tensor(B("mz")[:, :], B("AC")[:, 0:128], B("AC")[:, 128:256], A.max), (R("AC"),), (R("mz"),))
+    zs = 128 * n
+
+    def fz():
+        mm(P(0)[:, 0:128], sl("ID"), z, True, False)
+        return mm(P(0)[:, 0:128], sl("NID"), B("mz")[:, :], False, True)
+    add("T", tt(128, 2), fz, (rz, R("mz"), rs("ID"), rs("NID")), (PR(0),))
+    add("S", vt(128), lambda: S.activation(T.ZS[:, zs:zs + 128], P(0)[:, 0:128], AF.Abs, bias=256.0), (PR(0),), (("ZS", zs, zs + 128),))
+    if not last:
+        nz = 512 * (n + 2)
+
+        def sendz():
+            return g.remote_dma(out_ap=T.Z4[:, nz:nz + 128], in_ap=T.ZS[:, zs:zs + 128], remote_sem=T.sem["az%d_%d" % (e + 1, c)],
+                                local_sem=T.sem.loc, pid=pid, routing_id=rid, dma_engine_mask=emask)
+        sz = add("G", 1.0, sendz, (("ZS", zs, zs + 128),), (), kind="s")
+        _lead_sends[(e, c)] = (sh, sz)
+    else:
+        add("Y", .1, lambda: SY.dma_start(T.yz[:, 128 * c:128 * c + 128], T.ZS[:, zs:zs + 128]), (("ZS", zs, zs + 128),), (),
+            kind="d", sem="st%d" % (4 + c), val=16, lat=2.2)
+
+
+_lead_sends = {}

@@ -5,7 +5,7 @@ from concourse.mybir import dt, AluOpType, AxisListType, ActivationFunctionType
 A = AluOpType
 AF = ActivationFunctionType
 LE = 6
-SLOTS = ["ones", "BD0", "BD", "ID", "ID64", "NID", "IDm32", "IDh", "TGE", "SLT", "SD0", "SD", "NBD", "NSLT", "ID16",
+SLOTS = ["ones", "BD0", "BD", "ID", "ID64", "NID", "IDm32", "IDh", "TGE", "SLT", "SGT", "SD0", "SD", "NBD", "NSLT", "ID16",
          "ID64t", "DE", "DX", "DK", "DKL"]
 
 SCRATCH = {
@@ -18,7 +18,7 @@ SCRATCH = {
     "TB": ("sbuf", [128, 128 * len(SLOTS)], "bfloat16"),
     "IDF": ("sbuf", [128, 128], "float32"), "ONE16": ("sbuf", [128, 128], "float32"),
     "L1": ("sbuf", [128, 2048], "bfloat16"), "L2": ("sbuf", [128, 2048], "bfloat16"),
-    "PQ": ("sbuf", [128, 2048], "float16"), "WL": ("sbuf", [128, 2048], "bfloat16"),
+    "PQ": ("sbuf", [128, 2048], "bfloat16"), "WL": ("sbuf", [128, 2048], "bfloat16"),
     "W37": ("sbuf", [128, 128], "float16"),
     "COL": ("sbuf", [128, 16], "float32"), "kk": ("sbuf", [128, 16], "float32"), "RK": ("sbuf", [128, 16], "float32"),
     "rowi": ("sbuf", [128, 2], "int32"), "r15": ("sbuf", [128, 2], "int32"),
@@ -48,7 +48,13 @@ CY = 0.83e-3 * 1.25
 TC = 0.42e-3 * 1.25
 GAT = 1.55
 SCA = 3.8
-HOP = 0.06
+YS = ()
+NOISE, SEED, WIN, BON = 0.0, 0, 0.02, 0.0
+_OFF = [
+    [15, 31, -2, -25, 55, 35, 8, 160, 63, 53, 15, 11, 25, 37, -30, 33, -3, 8, 48, 22, 15, 7, 8, 30, -5, -6, 11, 52, 2, 83, -6, 11, -5, 40, 8, -23, 61, 98, 2, 36, 32, 67, 21, 54, 23, 37, 62, 43, 47, 44, -12, -25, 18, 67, -4, 64, 35, 31, -69, 33, 9, 51, -23, 46, -6, 24, 10, 77, 36, -46, -65, 60, 31, 47, -6, 19, 2, 11, 23, 23, -11, 9, -34, -43, -11, -13, -20, 25, 21, 65, 4, 31, 1, 52, -15, 51, -57, 30, -74, -30, 44, 28, 22, 10, -43, -3, -24, 33, 14, 65, 18, 0, -13, 4],
+    [-42, -73, 42, 3, 40, 4, -27, 28, 27, -103, -24, 68, 5, 34, 66, -27, -22, -38, 24, -14, -14, -24, -21, -40, -40, 47, -2, 35, 23, -30, -84, -68, -82, -70, -72, -72, 35, -51, -108, -26, -28, -25, -65, -80, -5, -54, -111, -32, -11, -69, -6, -24, -20, 36, -80, -14, -111, 33, 50, 68, 2, 45, 26, 24, 92, 84, 105, -5, 38, -4, 16, 17, 14, 23, 6, 19, 43, 4, 9, 4, -1, 103, 6, 30, -3, -1, 23, 46, 13, -2, -28, -73, 0, -79, -50, 11, -48, -12, -13, 8, 7, 5, -16, -5, 67, -46, -49, -5, 11, 30, -48, 82, -67, -41, -64]]
+OFFS = {(_c, _i): float(_v) for _c in range(2) for _i, _v in enumerate(_OFF[_c])}
+HOP = 0.08
 
 
 def rank_program(g, core, T, topo):
@@ -65,6 +71,7 @@ def rank_program(g, core, T, topo):
     V, S, TE, SY = g.vector, g.scalar, g.tensor, g.sync
     QS = {"V": V, "S": S, "T": TE, "G": g, "Y": SY}
     ops, acc = [], {}
+    cur = [-1, -1, 0]
 
     def add(q, dur, emit, R=(), W=(), kind="c", sem=None, val=0, lat=0.0, extra=()):
         i = len(ops)
@@ -95,7 +102,8 @@ def rank_program(g, core, T, topo):
                     keep.append(a)
                 keep.append((i, lo, hi, isw))
                 acc[buf] = keep
-        ops.append({"q": q, "dur": dur, "emit": emit, "deps": deps, "kind": kind, "sem": sem, "val": val, "lat": lat})
+        ops.append({"q": q, "dur": dur, "emit": emit, "deps": deps, "kind": kind, "sem": sem, "val": val, "lat": lat,
+                    "key": (cur[0], cur[1], i - cur[2])})
         return i
 
     def vt(n, rate=1.0):
@@ -163,12 +171,14 @@ def rank_program(g, core, T, topo):
     add("V", vt(8), lambda: ts(T.I4[:, :], T.I4a[:, :], col(10), None, A.add), (("I4a", 0, 8), rc(10)), (("I4", 0, 8),))
 
     def scl(o, i, a):
-        add("V", vt(128, .5), lambda: ts(sl(o), sl(i), float(a), None, A.mult), (rs(i),), (rs(o),))
+        add("S", vt(128), lambda: S.activation(sl(o), sl(i), AF.Copy, scale=float(a)), (rs(i),), (rs(o),))
     scl("ID64", "ID", 64)
     add("V", vt(2048, .5), lambda: V.memset(T.L1[:, :], 0.0), (), (("L1", 0, 2048),))
 
     def cpy(buf, base, off, src):
-        add("V", vt(8), lambda: V.tensor_copy(T[buf][:, base + off:base + 128:16], T.TB[:, 128 * SLOTS.index(src) + off:128 * SLOTS.index(src) + 128:16]), (rs(src),), ((buf, base + off, base + off + 113),))
+        a = 128 * SLOTS.index(src)
+        add("S", vt(8), lambda: S.activation(T[buf][:, base + off:base + 128:16], T.TB[:, a + off:a + 128:16], AF.Copy),
+            (rs(src),), ((buf, base + off, base + off + 113),))
     for k in range(16):
         cpy("L1", 128 * k, k, "BD")
     add("V", vt(2048, .5), lambda: ts(T.WL[:, :], T.L1[:, :], T.wtb[:, 0:1], None, A.mult), (("L1", 0, 2048), ("wtb", 0, 1)), (("WL", 0, 2048),))
@@ -206,24 +216,23 @@ def rank_program(g, core, T, topo):
     scl("ID16", "ID", 1 / 16)
     scl("ID64t", "ID", 1 / 64)
     scl("NBD", "BD", -1)
-    add("V", vt(128, 2), lambda: V.tensor_tensor(sl("SLT"), sl("BD"), sl("TGE"), A.subtract), (rs("BD"), rs("TGE")), (rs("SLT"),))
-    add("V", vt(128, 2), lambda: V.tensor_tensor(sl("SD0"), sl("SLT"), sl("TGE"), A.subtract), (rs("SLT"), rs("TGE")), (rs("SD0"),))
-    add("V", vt(128, 2), lambda: V.tensor_tensor(sl("SD0"), sl("SD0"), sl("ID"), A.add), (rs("SD0"), rs("ID")), (rs("SD0"),))
+    add("G", .4, lambda: g.affine_select(sl("SLT"), sl("BD"), [[1, 128]], A.is_ge, 0.0, -1, -1), (rs("BD"),), (rs("SLT"),))
+    add("G", .4, lambda: g.affine_select(sl("SGT"), sl("BD"), [[-1, 128]], A.is_ge, 0.0, -1, 1), (rs("BD"),), (rs("SGT"),))
+    add("V", vt(128, 2), lambda: V.tensor_tensor(sl("SD0"), sl("SLT"), sl("SGT"), A.subtract), (rs("SLT"), rs("SGT")), (rs("SD0"),))
     scl("SD", "SD0", 1 / 1024)
     scl("NSLT", "SLT", -1 / 16)
     for nm, ci in (("DE", 1), ("DX", 2), ("DK", 3), ("DKL", 4)):
         def dg(nm=nm, ci=ci):
-            add("V", vt(128, .5), lambda: ts(sl(nm), sl("ID"), col(ci), None, A.mult), (rs("ID"), rc(ci)), (rs(nm),))
+            add("S", vt(128), lambda: S.activation(sl(nm), sl("ID"), AF.Copy, scale=col(ci)), (rs("ID"), rc(ci)), (rs(nm),))
         dg()
     add("V", vt(128), lambda: V.memset(T.ONE16[:, :], 16.0), (), (("ONE16", 0, 128),))
-    add("V", vt(16), lambda: ts(T.RK[:, :], T.kk[:, :], col(0), None, A.is_equal), (("kk", 0, 16), rc(0)), (("RK", 0, 16),))
+    add("V", vt(16), lambda: ts(T.RK[:, :], T.kk[:, :], col(0), 256.0, A.is_equal, A.mult), (("kk", 0, 16), rc(0)), (("RK", 0, 16),))
     for k in range(16):
         def l2(k=k):
-            add("V", vt(128, .5), lambda: ts(T.L2[:, 128 * k:128 * k + 128], sl("BD"), T.RK[:, k:k + 1], 256.0, A.mult, A.mult),
+            add("S", vt(128), lambda: S.activation(T.L2[:, 128 * k:128 * k + 128], sl("BD"), AF.Copy, scale=T.RK[:, k:k + 1]),
                 (rs("BD"), ("RK", 0, 16)), (("L2", 128 * k, 128 * k + 128),))
         l2()
-    add("V", vt(2048, .5), lambda: V.tensor_scalar(T.CL0[:, 0:2048], T.L1[:, :], 0.0, None, A.mult), (("L1", 0, 2048),), (("CL0", 0, 2048),))
-    add("V", vt(2048, .5), lambda: V.tensor_copy(T.PQ[:, :], T.CL0[:, 0:2048]), (("CL0", 0, 2048),), (("PQ", 0, 2048),))
+    add("V", vt(2048, .5), lambda: V.memset(T.PQ[:, :], 0.0), (), (("PQ", 0, 2048),))
     for k in range(16):
         cpy("PQ", 128 * k, k, "BD")
         if k < 15:
@@ -231,6 +240,7 @@ def rank_program(g, core, T, topo):
 
     for e in range(LE):
         for c in range(2):
+            cur[0], cur[1], cur[2] = e, c, len(ops) + (0 if e else -2)
             _lead(e, c, T, g, V, S, TE, SY, add, vt, tt, sl, rs, col, rc, mm, ts, rid, pid, emask, neng, ops)
 
     n = len(ops)
@@ -244,6 +254,9 @@ def rank_program(g, core, T, topo):
     for i in range(n - 1, -1, -1):
         o = ops[i]
         tail[i] = o["dur"] + o["lat"] + max([tail[k] + HOP for k in succ[i]] + [0.0])
+    rng = np.random.RandomState(SEED)
+    for i in range(n):
+        tail[i] = tail[i] + NOISE * float(rng.rand()) + (OFFS.get(ops[i]["key"][1:], 0.0) if ops[i]["key"][0] >= 0 else 0.0)
     free = {}
     ready = [0.0] * n
     cand = {}
@@ -258,7 +271,7 @@ def rank_program(g, core, T, topo):
                 continue
             fq = free.get(q, 0.0)
             st = min(max(fq, ready[i]) for i in lst)
-            pick = max((i for i in lst if max(fq, ready[i]) <= st + 0.02), key=lambda i: (tail[i], -i))
+            pick = max((i for i in lst if max(fq, ready[i]) <= st + WIN), key=lambda i: (tail[i], -i))
             if best is None or st < best[0]:
                 best = (st, q, pick)
         if best is None:
@@ -274,7 +287,8 @@ def rank_program(g, core, T, topo):
         end += ops[i]["lat"]
         order.append(i)
         for k in succ[i]:
-            ready[k] = max(ready[k], end + HOP)
+            inorder = ops[k]["q"] == q and not ops[k]["deps"][i]
+            ready[k] = max(ready[k], end if inorder else end + HOP)
             cnt[k] -= 1
             if cnt[k] == 0:
                 cand.setdefault(ops[k]["q"], []).append(k)
@@ -380,42 +394,60 @@ def _lead(e, c, T, g, V, S, TE, SY, add, vt, tt, sl, rs, col, rc, mm, ts, rid, p
     add("V", vt(128), lambda: V.tensor_tensor(B("s1")[:, :], B("pr")[:, :], P(7)[:, 256:384], A.add), (R("pr"), PR(7)), (R("s1"),))
     add("V", vt(128), lambda: ts(B("s2")[:, :], B("s1")[:, :], 4095, None, A.bitwise_and), (R("s1"),), (R("s2"),))
     add("V", vt(128), lambda: V.tensor_copy(B("s16")[:, :], B("s2")[:, :]), (R("s2"),), (R("s16"),))
-    for hf in range(2):
+    for hf in range(4):
         def fx(hf=hf):
-            return S.activation(B("x")[:, 1024 * hf:1024 * hf + 1024], T.X[:, :].indirect(B("K16")[:, 64 * hf:64 * hf + 64]), AF.Copy)
-        add("S", vt(1024, GAT), fx, (R("K16"), ("X", 0, 4096)), (R("x", 1024 * hf, 1024 * hf + 1024),))
+            return S.activation(B("x")[:, 512 * hf:512 * hf + 512], T.X[:, :].indirect(B("K16")[:, 32 * hf:32 * hf + 32]), AF.Copy)
+        add("S", vt(512, GAT), fx, (R("K16"), ("X", 0, 4096)), (R("x", 512 * hf, 512 * hf + 512),))
     add("S", vt(128, GAT), lambda: S.activation(B("Wo")[:, :], T.Wf[:, wa:wb].indirect(B("c16")[:, 0:8]), AF.Copy),
         (R("c16"), ("Wf", wa, wb)), (R("Wo"),))
     add("V", vt(128), lambda: V.tensor_tensor(B("dk")[:, :], B("Wo")[:, :], Kp, A.subtract), (R("Wo"), PR(7)), (R("dk"),))
-    for hf in range(2):
-        a, b = 1024 * hf, 1024 * hf + 1024
+    for pc in range(4):
+        a, b = 512 * pc, 512 * pc + 512
+        yo = B("s16")[:, 32 * pc:32 * pc + 32]
+        if pc in YS:
+            bk = pc % 2
 
-        def fy(hf=hf, a=a, b=b):
-            return V.tensor_tensor(B("d")[:, a:b], T.Y[:, :].indirect(B("s16")[:, 64 * hf:64 * hf + 64]), B("x")[:, a:b], A.subtract)
-        add("V", vt(1024, GAT), fy, (R("s16"), ("Y", 0, 4096), R("x", a, b)), (R("d", a, b),))
+            def fy(a=a, b=b, yo=yo):
+                return S.activation(B("d")[:, a:b], T.Y[:, :].indirect(yo), AF.Copy)
+            add("S", vt(512, GAT), fy, (R("s16"), ("Y", 0, 4096)), (R("d", a, b),))
 
-        def fa(a=a, b=b):
-            return S.activation(B("d")[:, a:b], B("d")[:, a:b], AF.Abs)
-        add("S", vt(1024), fa, (R("d", a, b),), (R("d", a, b),))
+            def fd(a=a, b=b, bk=bk):
+                mm(P(bk)[:, 0:512], sl("NID"), B("x")[:, a:b], True, False)
+                return mm(P(bk)[:, 0:512], sl("ID"), B("d")[:, a:b], False, True)
+            add("T", tt(512, 2), fd, (R("x", a, b), R("d", a, b), rs("ID"), rs("NID")), (PR(bk),))
+            add("S", vt(512), lambda a=a, b=b, bk=bk: S.activation(B("d")[:, a:b], P(bk)[:, 0:512], AF.Abs), (PR(bk),), (R("d", a, b),))
+        else:
+            def fy(a=a, b=b, yo=yo):
+                return V.tensor_tensor(B("d")[:, a:b], T.Y[:, :].indirect(yo), B("x")[:, a:b], A.subtract)
+            add("V", vt(512, GAT), fy, (R("s16"), ("Y", 0, 4096), R("x", a, b)), (R("d", a, b),))
 
-        def fD(hf=hf, a=a, b=b):
-            for k in range(16):
-                i = mm(P(4)[:, 64 * hf:64 * hf + 64], T.L1[:, 128 * k:128 * k + 128], B("d")[:, a + k:b:16], k == 0, k == 15)
-            return i
-        add("T", tt(64, 16), fD, (R("d", a, b), ("L1", 0, 2048)), (PR(4),))
+            def fa(a=a, b=b):
+                return S.activation(B("d")[:, a:b], B("d")[:, a:b], AF.Abs)
+            add("S", vt(512), fa, (R("d", a, b),), (R("d", a, b),))
+        if pc % 2:
+            hf = pc // 2
+
+            def fD(hf=hf):
+                a, b = 1024 * hf, 1024 * hf + 1024
+                for k in range(16):
+                    i = mm(P(4)[:, 64 * hf:64 * hf + 64], T.L1[:, 128 * k:128 * k + 128], B("d")[:, a + k:b:16], k == 0, k == 15)
+                return i
+            add("T", tt(64, 16), fD, (R("d", 1024 * hf, 1024 * hf + 1024), ("L1", 0, 2048)), (PR(4),))
     for bk in range(4):
-        def fb(bk=bk):
-            mm(P(bk)[:, 0:512], sl("NID"), T.Z4[:, zb:zb + 512], True, False)
+        pb = bk % 2
+
+        def fb(bk=bk, pb=pb):
+            mm(P(pb)[:, 0:512], sl("NID"), T.Z4[:, zb:zb + 512], True, False)
             for j in range(4):
-                i = mm(P(bk)[:, 128 * j:128 * j + 128], sl("ID"), B("x")[:, 4 * bk + j:2048:16], False, j == 3)
+                i = mm(P(pb)[:, 128 * j:128 * j + 128], sl("ID"), B("x")[:, 4 * bk + j:2048:16], False, j == 3)
             return i
-        add("T", tt(512, 2), fb, (("Z4", zb, zb + 512), R("x"), rs("ID"), rs("NID")), (PR(bk),))
+        add("T", tt(512, 2), fb, (("Z4", zb, zb + 512), R("x"), rs("ID"), rs("NID")), (PR(pb),))
         for j in range(2):
             pr = 2 * bk + j
 
-            def fs(bk=bk, j=j, pr=pr):
+            def fs(bk=pb, j=j, pr=pr):
                 return S.activation(B("sg")[:, 256 * pr:256 * pr + 256], P(bk)[:, 256 * j:256 * j + 256], AF.Sign, bias=0.5 - 16.0 * (7 - pr))
-            add("S", vt(256), fs, (PR(bk),), (R("sg", 256 * pr, 256 * pr + 256),))
+            add("S", vt(256), fs, (PR(pb),), (R("sg", 256 * pr, 256 * pr + 256),))
     for bk in range(4):
         def fc(bk=bk):
             for j in range(4):
@@ -511,28 +543,30 @@ def _lead(e, c, T, g, V, S, TE, SY, add, vt, tt, sl, rs, col, rc, mm, ts, rid, p
     if last:
         add("Y", .1, lambda: SY.dma_start(T.yw[:, wa:wb], T.Wf[:, wa:wb]), (("Wf", wa, wb),), (), kind="d", sem="st%d" % (2 + c), val=16, lat=2.5)
     for bk in range(4):
-        def fm(bk=bk):
+        pb = 2 + bk % 2
+
+        def fm(bk=bk, pb=pb):
             for j in range(4):
                 k = 4 * bk + j
-                mm(P(bk)[:, 128 * j:128 * j + 128], sl("ID"), B("x")[:, k:2048:16], True, False)
-                i = mm(P(bk)[:, 128 * j:128 * j + 128], T.L2[:, 128 * k:128 * k + 128], h, False, True)
+                mm(P(pb)[:, 128 * j:128 * j + 128], sl("ID"), B("x")[:, k:2048:16], True, False)
+                i = mm(P(pb)[:, 128 * j:128 * j + 128], T.L2[:, 128 * k:128 * k + 128], h, False, True)
             return i
-        add("T", tt(128, 8), fm, (R("h"), R("x"), ("L2", 0, 2048), rs("ID")), (PR(bk),))
+        add("T", tt(128, 8), fm, (R("h"), R("x"), ("L2", 0, 2048), rs("ID")), (PR(pb),))
         for j in range(2):
-            def fM(bk=bk, j=j):
-                src = P(bk)[:, 256 * j:256 * j + 256]
+            def fM(bk=bk, j=j, pb=pb):
+                src = P(pb)[:, 256 * j:256 * j + 256]
                 if bk == 0 and j == 0:
                     return ts(B("AC")[:, :], src, 256.0, None, A.max)
                 return V.tensor_tensor(B("AC")[:, :], B("AC")[:, :], src, A.max)
-            add("V", vt(256), fM, (PR(bk),) if bk == 0 and j == 0 else (R("AC"), PR(bk)), (R("AC"),))
+            add("V", vt(256), fM, (PR(pb),) if bk == 0 and j == 0 else (R("AC"), PR(pb)), (R("AC"),))
     add("V", vt(128, 2), lambda: V.tensor_tensor(B("mz")[:, :], B("AC")[:, 0:128], B("AC")[:, 128:256], A.max), (R("AC"),), (R("mz"),))
     zs = 128 * n
 
     def fz():
-        mm(P(0)[:, 0:128], sl("ID"), z, True, False)
-        return mm(P(0)[:, 0:128], sl("NID"), B("mz")[:, :], False, True)
-    add("T", tt(128, 2), fz, (rz, R("mz"), rs("ID"), rs("NID")), (PR(0),))
-    add("S", vt(128), lambda: S.activation(T.ZS[:, zs:zs + 128], P(0)[:, 0:128], AF.Abs, bias=256.0), (PR(0),), (("ZS", zs, zs + 128),))
+        mm(P(2)[:, 0:128], sl("ID"), z, True, False)
+        return mm(P(2)[:, 0:128], sl("NID"), B("mz")[:, :], False, True)
+    add("T", tt(128, 2), fz, (rz, R("mz"), rs("ID"), rs("NID")), (PR(2),))
+    add("S", vt(128), lambda: S.activation(T.ZS[:, zs:zs + 128], P(2)[:, 0:128], AF.Abs, bias=256.0), (PR(2),), (("ZS", zs, zs + 128),))
     if not last:
         nz = 512 * (n + 2)
 

import numpy as np
from concourse.bass import DstId, RemoteDMATransfer
from concourse.mybir import dt, AluOpType, AxisListType, ActivationFunctionType

A = AluOpType
AF = ActivationFunctionType
LE = 6
SLOTS = ["ones", "BD0", "BD", "ID", "ID64", "NID", "IDm32", "IDh", "TGE", "SLT", "SGT", "SD0", "SD", "NBD", "NSLT", "ID16",
         "ID64t", "DE", "DX", "DK", "DKL"]

SCRATCH = {
    "X": ("sbuf", [128, 4096], "bfloat16"), "Y": ("sbuf", [128, 4096], "bfloat16"),
    "Gf": ("sbuf", [128, 1024], "float32"), "Wf": ("sbuf", [128, 1024], "float32"),
    "rti": ("sbuf", [128, 1024], "int32"), "wri": ("sbuf", [128, 1024], "int32"), "rki": ("sbuf", [128, 256], "int32"),
    "thi": ("sbuf", [128, 1], "int32"), "wtb": ("sbuf", [128, 1], "bfloat16"),
    "Z4": ("sbuf", [128, 12 * 512], "bfloat16"), "HL": ("sbuf", [128, 12 * 256], "bfloat16"),
    "HS": ("sbuf", [128, 12 * 256], "bfloat16"), "ZS": ("sbuf", [128, 12 * 128], "bfloat16"),
    "TB": ("sbuf", [128, 128 * len(SLOTS)], "bfloat16"),
    "IDF": ("sbuf", [128, 128], "float32"), "ONE16": ("sbuf", [128, 128], "float32"),
    "L1": ("sbuf", [128, 2048], "bfloat16"), "L2": ("sbuf", [128, 2048], "bfloat16"),
    "PQ": ("sbuf", [128, 2048], "bfloat16"), "WL": ("sbuf", [128, 2048], "bfloat16"),
    "W37": ("sbuf", [128, 128], "float16"),
    "COL": ("sbuf", [128, 16], "float32"), "kk": ("sbuf", [128, 16], "float32"), "RK": ("sbuf", [128, 16], "float32"),
    "rowi": ("sbuf", [128, 2], "int32"), "r15": ("sbuf", [128, 2], "int32"),
    "I4a": ("sbuf", [128, 8], "int32"), "I4": ("sbuf", [128, 8], "int32"),
    "Fi": ("sbuf", [128, 1], "int32"), "Fj": ("sbuf", [128, 1], "int32"),
    "YK": ("sbuf", [128, 256], "float32"), "hI": ("sbuf", [128, 256], "int32"), "lI": ("sbuf", [128, 256], "int32"),
}
for _c in range(2):
    for _n, _w, _d in (("K16", 128, "uint16"), ("x", 2048, "bfloat16"), ("d", 2048, "bfloat16"), ("sg", 2048, "bfloat16"),
                       ("ua", 8, "int32"), ("ub", 8, "int32"), ("uc", 8, "int32"), ("ud", 8, "int32"), ("ue", 8, "int32"),
                       ("c16", 8, "uint16"), ("Gs", 128, "float32"), ("Wo", 128, "float32"), ("dk", 128, "float32"),
                       ("dl", 128, "float32"), ("val", 128, "float32"), ("p1", 128, "int32"), ("pr", 128, "int32"),
                       ("s1", 128, "int32"), ("s2", 128, "int32"), ("s16", 128, "uint16"), ("o", 128, "bfloat16"),
                       ("hd", 128, "bfloat16"), ("eo", 128, "bfloat16"), ("f", 128, "bfloat16"), ("h", 128, "bfloat16"),
                       ("m", 128, "bfloat16"), ("h64", 128, "bfloat16"), ("WW", 256, "float16"),
                       ("CL", 15 * 256, "float16"), ("AC", 256, "float16"), ("mz", 128, "float16"), ("Fs", 1, "float32")):
        SCRATCH[_n + str(_c)] = ("sbuf", [128, _w], _d)
for _b in range(8):
    SCRATCH["ps%d" % _b] = ("psum", [128, 512], "float32")

SEMAPHORES = ["eV", "eS", "eT", "eG", "loc"] + ["ld%d" % _i for _i in range(20)] + ["st%d" % _i for _i in range(8)]
for _e in range(LE):
    for _c in range(2):
        SEMAPHORES += ["zr%d_%d" % (_e, _c), "ah%d_%d" % (_e, _c), "az%d_%d" % (_e, _c)]

CY = 0.83e-3 * 1.25
TC = 0.42e-3 * 1.25
GAT = 1.55
SCA = 3.8
YS = ()
NOISE, SEED, WIN, BON = 0.0, 0, 0.02, 0.0
_OFF = [
    [15, 31, -2, -25, 55, 35, 8, 160, 63, 53, 15, 11, 25, 37, -30, 33, -3, 8, 48, 22, 15, 7, 8, 30, -5, -6, 11, 52, 2, 83, -6, 11, -5, 40, 8, -23, 61, 98, 2, 36, 32, 67, 21, 54, 23, 37, 62, 43, 47, 44, -12, -25, 18, 67, -4, 64, 35, 31, -69, 33, 9, 51, -23, 46, -6, 24, 10, 77, 36, -46, -65, 60, 31, 47, -6, 19, 2, 11, 23, 23, -11, 9, -34, -43, -11, -13, -20, 25, 21, 65, 4, 31, 1, 52, -15, 51, -57, 30, -74, -30, 44, 28, 22, 10, -43, -3, -24, 33, 14, 65, 18, 0, -13, 4],
    [-42, -73, 42, 3, 40, 4, -27, 28, 27, -103, -24, 68, 5, 34, 66, -27, -22, -38, 24, -14, -14, -24, -21, -40, -40, 47, -2, 35, 23, -30, -84, -68, -82, -70, -72, -72, 35, -51, -108, -26, -28, -25, -65, -80, -5, -54, -111, -32, -11, -69, -6, -24, -20, 36, -80, -14, -111, 33, 50, 68, 2, 45, 26, 24, 92, 84, 105, -5, 38, -4, 16, 17, 14, 23, 6, 19, 43, 4, 9, 4, -1, 103, 6, 30, -3, -1, 23, 46, 13, -2, -28, -73, 0, -79, -50, 11, -48, -12, -13, 8, 7, 5, -16, -5, 67, -46, -49, -5, 11, 30, -48, 82, -67, -41, -64]]
OFFS = {(_c, _i): float(_v) for _c in range(2) for _i, _v in enumerate(_OFF[_c])}
HOP = 0.08


def rank_program(g, core, T, topo):
    rank = T.rank_of(core)
    if rank is None:
        return
    cores = list(T.cores)
    dst = cores[(rank + 1) % len(cores)]
    rid, pid, _s = topo.addr(dst)
    engines = topo.engines(core, dst)
    emask = topo.mask(core, dst)
    neng = len(engines)

    V, S, TE, SY = g.vector, g.scalar, g.tensor, g.sync
    QS = {"V": V, "S": S, "T": TE, "G": g, "Y": SY}
    ops, acc = [], {}
    cur = [-1, -1, 0]

    def add(q, dur, emit, R=(), W=(), kind="c", sem=None, val=0, lat=0.0, extra=()):
        i = len(ops)
        deps = {}
        for j in extra:
            deps[j] = False
        for isw, regs in ((False, R), (True, W)):
            for buf, lo, hi in regs:
                lst = acc.setdefault(buf, [])
                ps = buf[:2] == "ps"
                keep = []
                for a in lst:
                    j, l, h, aw = a
                    if j == i:
                        keep.append(a)
                        continue
                    over = ps or (l < hi and lo < h)
                    same = ops[j]["q"] == q and ops[j]["kind"] == "c" and kind == "c"
                    if over:
                        if ps:
                            deps[j] = deps.get(j, False) or not same
                        elif isw or aw:
                            deps[j] = deps.get(j, False) or (aw if same else True)
                    if ps and same:
                        continue
                    if isw and (not ps) and l >= lo and h <= hi:
                        continue
                    keep.append(a)
                keep.append((i, lo, hi, isw))
                acc[buf] = keep
        ops.append({"q": q, "dur": dur, "emit": emit, "deps": deps, "kind": kind, "sem": sem, "val": val, "lat": lat,
                    "key": (cur[0], cur[1], i - cur[2])})
        return i

    def vt(n, rate=1.0):
        return 0.03 + max(64, n * rate) * CY

    def tt(n, cnt=1, f=1):
        return 0.02 + cnt * max(64, n) * TC * f

    def sl(n):
        s = SLOTS.index(n)
        return T.TB[:, 128 * s:128 * s + 128]

    def rs(n):
        s = SLOTS.index(n)
        return ("TB", 128 * s, 128 * s + 128)

    def col(i):
        return T.COL[:, i:i + 1]

    def rc(i):
        return ("COL", i, i + 1)

    def mm(o, l, r, a, b):
        return TE.matmul(o, l, r, a, b)

    def ts(out, in0, s1, s2, op0, op1=None):
        if op1 is None:
            return V.tensor_scalar(out, in0, s1, None, op0)
        return V.tensor_scalar(out, in0, s1, s2, op0, op1)

    nld = [0]

    def load(q, out, in_, reg, dur, lat):
        s = "ld%d" % nld[0]
        nld[0] += 1
        eng = QS[q]
        add(q, dur, lambda: eng.dma_start(out, in_), (), (reg,), kind="d", sem=s, val=16, lat=lat)

    load("Y", T.rki[:, :], T.rk[:, :], ("rki", 0, 256), 0.1, 2.2)
    load("S", T.Z4[:, 0:128], T.z0[:, 0:128], ("Z4", 0, 128), 0.1, 2.2)
    load("S", T.wtb[:, :], T.wt[:, :], ("wtb", 0, 1), 0.1, 2.2)
    load("Y", T.rti[:, 0:512], T.rt[:, 0:512], ("rti", 0, 512), 0.1, 3.5)
    load("S", T.X[:, :], T.gx[:, :], ("X", 0, 4096), 0.1, 6.5)
    load("S", T.Z4[:, 512:640], T.z0[:, 128:256], ("Z4", 512, 640), 0.1, 6.5)
    load("Y", T.Y[:, :], T.sy[:, :], ("Y", 0, 4096), 0.1, 9.5)
    load("Y", T.thi[:, :], T.th[:, :], ("thi", 0, 1), 0.1, 9.5)
    load("Y", T.wri[:, 0:512], T.wr[:, 0:512], ("wri", 0, 512), 0.1, 10.5)
    load("Y", T.rti[:, 512:1024], T.rt[:, 512:1024], ("rti", 512, 1024), 0.1, 11.5)
    load("Y", T.wri[:, 512:1024], T.wr[:, 512:1024], ("wri", 512, 1024), 0.1, 12.5)

    add("V", vt(128, .5), lambda: V.memset(sl("ones"), 1.0), (), (rs("ones"),))
    add("G", .4, lambda: g.iota(T.rowi[:, 0:1], [[0, 1]], 0, 1), (), (("rowi", 0, 1),))
    add("G", .4, lambda: g.affine_select(sl("BD0"), sl("ones"), [[-16, 8], [0, 16]], A.is_ge, 0.0, 0, 1), (rs("ones"),), (rs("BD0"),))
    add("G", .4, lambda: g.affine_select(sl("BD"), sl("BD0"), [[16, 8], [0, 16]], A.is_ge, 0.0, 15, -1), (rs("BD0"),), (rs("BD"),))
    add("G", .4, lambda: g.affine_select(sl("ID"), sl("ones"), [[-1, 128]], A.is_equal, 0.0, 0, 1), (rs("ones"),), (rs("ID"),))
    add("G", .2, lambda: g.iota(T.I4a[:, :], [[64, 8]], 0, 0), (), (("I4a", 0, 8),))
    add("G", .2, lambda: g.iota(T.kk[:, :], [[1, 16]], 0, 0, allow_small_or_imprecise_dtypes=True), (), (("kk", 0, 16),))
    add("G", .4, lambda: g.affine_select(sl("TGE"), sl("BD"), [[-1, 128]], A.is_ge, 0.0, 0, 1), (rs("BD"),), (rs("TGE"),))
    add("V", vt(1), lambda: ts(T.r15[:, 0:1], T.rowi[:, 0:1], 15, None, A.bitwise_and), (("rowi", 0, 1),), (("r15", 0, 1),))
    add("V", vt(1), lambda: V.tensor_copy(col(0), T.r15[:, 0:1]), (("r15", 0, 1),), (rc(0),))

    def lin(o, i, a, b):
        add("V", vt(1), lambda: ts(col(o), col(i), float(a), float(b), A.mult, A.add), (rc(i),), (rc(o),))
    lin(10, 0, 4, 0)
    add("V", vt(8), lambda: ts(T.I4[:, :], T.I4a[:, :], col(10), None, A.add), (("I4a", 0, 8), rc(10)), (("I4", 0, 8),))

    def scl(o, i, a):
        add("S", vt(128), lambda: S.activation(sl(o), sl(i), AF.Copy, scale=float(a)), (rs(i),), (rs(o),))
    scl("ID64", "ID", 64)
    add("V", vt(2048, .5), lambda: V.memset(T.L1[:, :], 0.0), (), (("L1", 0, 2048),))

    def cpy(buf, base, off, src):
        a = 128 * SLOTS.index(src)
        add("S", vt(8), lambda: S.activation(T[buf][:, base + off:base + 128:16], T.TB[:, a + off:a + 128:16], AF.Copy),
            (rs(src),), ((buf, base + off, base + off + 113),))
    for k in range(16):
        cpy("L1", 128 * k, k, "BD")
    add("V", vt(2048, .5), lambda: ts(T.WL[:, :], T.L1[:, :], T.wtb[:, 0:1], None, A.mult), (("L1", 0, 2048), ("wtb", 0, 1)), (("WL", 0, 2048),))
    add("V", vt(1), lambda: ts(col(7), T.wtb[:, 0:1], 37.0, None, A.mult), (("wtb", 0, 1),), (rc(7),))
    add("V", vt(1), lambda: ts(col(8), col(7), 2048.0, -4096.0, A.is_gt, A.mult), (rc(7),), (rc(8),))
    add("V", vt(1), lambda: V.tensor_tensor(col(9), col(7), col(8), A.add), (rc(7), rc(8)), (rc(9),))
    add("V", vt(128, .5), lambda: ts(T.W37[:, :], sl("BD"), col(9), None, A.mult), (rs("BD"), rc(9)), (("W37", 0, 128),))
    add("V", vt(128), lambda: V.tensor_copy(T.IDF[:, :], sl("ID")), (rs("ID"),), (("IDF", 0, 128),))

    def hl0(c):
        a, b = 128 * c, 128 * c + 128
        add("V", vt(128), lambda: ts(T.hI[:, a:b], T.rki[:, a:b], 6, None, A.arith_shift_right), (("rki", 0, 256),), (("hI", a, b),))
        add("V", vt(128), lambda: ts(T.lI[:, a:b], T.rki[:, a:b], 63, None, A.bitwise_and), (("rki", 0, 256),), (("lI", a, b),))
        add("V", vt(128), lambda: V.tensor_copy(T.HL[:, 256 * c:256 * c + 128], T.hI[:, a:b]), (("hI", a, b),), (("HL", 256 * c, 256 * c + 128),))
        add("V", vt(128), lambda: V.tensor_copy(T.HL[:, 256 * c + 128:256 * c + 256], T.lI[:, a:b]), (("lI", a, b),), (("HL", 256 * c + 128, 256 * c + 256),))
    hl0(0)
    hl0(1)

    def conv(dst_, src, c):
        a, b = 512 * c, 512 * c + 512
        add("V", vt(512), lambda: V.tensor_copy(T[dst_][:, a:b], T[src][:, a:b]), ((src, a, b),), ((dst_, a, b),))
    conv("Gf", "rti", 0)
    conv("Wf", "wri", 0)
    conv("Gf", "rti", 1)
    conv("Wf", "wri", 1)
    add("V", vt(1), lambda: V.tensor_copy(col(11), T.thi[:, 0:1]), (("thi", 0, 1),), (rc(11),))
    lin(1, 0, -1, 15)
    lin(2, 0, -2, 15)
    lin(3, 0, 64, 0)
    lin(4, 0, 64, 8256)
    lin(5, 0, 64, -960)
    scl("NID", "ID", -1)
    scl("IDm32", "ID", -1 / 32)
    scl("IDh", "ID", 0.5)
    scl("ID16", "ID", 1 / 16)
    scl("ID64t", "ID", 1 / 64)
    scl("NBD", "BD", -1)
    add("G", .4, lambda: g.affine_select(sl("SLT"), sl("BD"), [[1, 128]], A.is_ge, 0.0, -1, -1), (rs("BD"),), (rs("SLT"),))
    add("G", .4, lambda: g.affine_select(sl("SGT"), sl("BD"), [[-1, 128]], A.is_ge, 0.0, -1, 1), (rs("BD"),), (rs("SGT"),))
    add("V", vt(128, 2), lambda: V.tensor_tensor(sl("SD0"), sl("SLT"), sl("SGT"), A.subtract), (rs("SLT"), rs("SGT")), (rs("SD0"),))
    scl("SD", "SD0", 1 / 1024)
    scl("NSLT", "SLT", -1 / 16)
    for nm, ci in (("DE", 1), ("DX", 2), ("DK", 3), ("DKL", 4)):
        def dg(nm=nm, ci=ci):
            add("S", vt(128), lambda: S.activation(sl(nm), sl("ID"), AF.Copy, scale=col(ci)), (rs("ID"), rc(ci)), (rs(nm),))
        dg()
    add("V", vt(128), lambda: V.memset(T.ONE16[:, :], 16.0), (), (("ONE16", 0, 128),))
    add("V", vt(16), lambda: ts(T.RK[:, :], T.kk[:, :], col(0), 256.0, A.is_equal, A.mult), (("kk", 0, 16), rc(0)), (("RK", 0, 16),))
    for k in range(16):
        def l2(k=k):
            add("S", vt(128), lambda: S.activation(T.L2[:, 128 * k:128 * k + 128], sl("BD"), AF.Copy, scale=T.RK[:, k:k + 1]),
                (rs("BD"), ("RK", 0, 16)), (("L2", 128 * k, 128 * k + 128),))
        l2()
    add("V", vt(2048, .5), lambda: V.memset(T.PQ[:, :], 0.0), (), (("PQ", 0, 2048),))
    for k in range(16):
        cpy("PQ", 128 * k, k, "BD")
        if k < 15:
            cpy("PQ", 128 * k, k + 1, "NBD")

    for e in range(LE):
        for c in range(2):
            cur[0], cur[1], cur[2] = e, c, len(ops) + (0 if e else -2)
            _lead(e, c, T, g, V, S, TE, SY, add, vt, tt, sl, rs, col, rc, mm, ts, rid, pid, emask, neng, ops)

    n = len(ops)
    succ = [[] for _ in range(n)]
    cnt = [0] * n
    for i, o in enumerate(ops):
        for j in o["deps"]:
            succ[j].append(i)
        cnt[i] = len(o["deps"])
    tail = [0.0] * n
    for i in range(n - 1, -1, -1):
        o = ops[i]
        tail[i] = o["dur"] + o["lat"] + max([tail[k] + HOP for k in succ[i]] + [0.0])
    rng = np.random.RandomState(SEED)
    for i in range(n):
        tail[i] = tail[i] + NOISE * float(rng.rand()) + (OFFS.get(ops[i]["key"][1:], 0.0) if ops[i]["key"][0] >= 0 else 0.0)
    free = {}
    ready = [0.0] * n
    cand = {}
    for i in range(n):
        if cnt[i] == 0:
            cand.setdefault(ops[i]["q"], []).append(i)
    order = []
    while True:
        best = None
        for q, lst in cand.items():
            if not lst:
                continue
            fq = free.get(q, 0.0)
            st = min(max(fq, ready[i]) for i in lst)
            pick = max((i for i in lst if max(fq, ready[i]) <= st + WIN), key=lambda i: (tail[i], -i))
            if best is None or st < best[0]:
                best = (st, q, pick)
        if best is None:
            break
        _st, q, i = best
        cand[q].remove(i)
        start = max(free.get(q, 0.0), ready[i])
        if ops[i]["kind"] == "r":
            end = start
        else:
            end = start + ops[i]["dur"]
            free[q] = end
        end += ops[i]["lat"]
        order.append(i)
        for k in succ[i]:
            inorder = ops[k]["q"] == q and not ops[k]["deps"][i]
            ready[k] = max(ready[k], end if inorder else end + HOP)
            cnt[k] -= 1
            if cnt[k] == 0:
                cand.setdefault(ops[k]["q"], []).append(k)
    if len(order) != n:
        raise ValueError("cycle")

    count = {"V": 0, "S": 0, "T": 0, "G": 0}
    known = {q: {} for q in ("V", "S", "T", "G", "Y")}
    nsend = 0
    for i in order:
        o = ops[i]
        q = o["q"]
        if o["kind"] == "r":
            o["clk"] = {o["sem"]: o["val"]}
            continue
        kn = known[q]
        for j in sorted((j for j, w in o["deps"].items() if w), key=lambda j: -order.index(j) if False else -j):
            p = ops[j]
            if p["kind"] == "s":
                raise ValueError("nothing waits for a send")
            sem, val = (p["sem"], p["val"]) if p["kind"] != "c" else ("e" + p["q"], p["pos"])
            if kn.get(sem, 0) < val:
                QS[q].wait_ge(T.sem[sem], val)
                for s2, v2 in p["clk"].items():
                    if kn.get(s2, 0) < v2:
                        kn[s2] = v2
        ins = o["emit"]()
        clk = dict(kn)
        if o["kind"] == "c":
            count[q] += 1
            o["pos"] = count[q]
            ins.then_inc(T.sem["e" + q], 1)
            clk["e" + q] = count[q]
        elif o["kind"] == "d":
            if ins is not None:
                ins.then_inc(T.sem[o["sem"]], 16)
            clk[o["sem"]] = o["val"]
        else:
            nsend += 1
        o["clk"] = clk
    kn = known["Y"]
    for q in ("V", "S", "T", "G"):
        SY.wait_ge(T.sem["e" + q], count[q])
    for o in ops:
        if o["kind"] in ("d", "r"):
            if kn.get(o["sem"], 0) < o["val"]:
                SY.wait_ge(T.sem[o["sem"]], o["val"])
                kn[o["sem"]] = o["val"]
    g.wait_ge(T.sem.loc, neng * nsend)


def _lead(e, c, T, g, V, S, TE, SY, add, vt, tt, sl, rs, col, rc, mm, ts, rid, pid, emask, neng, ops):
    first, last = e == 0, e == LE - 1
    n = 2 * e + c
    B = lambda nm: T[nm + str(c)]
    R = lambda nm, a=0, b=None: (nm + str(c), a, b if b is not None else SCRATCH[nm + str(c)][1][1])
    P = lambda b: T["ps%d" % b]
    PR = lambda b: ("ps%d" % b, 0, 512)
    zb, hb = 512 * n, 256 * n
    z = T.Z4[:, zb:zb + 128]
    hi, lo = T.HL[:, hb:hb + 128], T.HL[:, hb + 128:hb + 256]
    rz, rhl = ("Z4", zb, zb + 128), ("HL", hb, hb + 256)
    if not first:
        sh, sz = _lead_sends[(e - 1, c)]
        add("R", 0, None, (), (rhl,), kind="r", sem="ah%d_%d" % (e, c), val=neng, lat=3.0, extra=(sh,))
        add("R", 0, None, (), (rz,), kind="r", sem="az%d_%d" % (e, c), val=neng, lat=3.0, extra=(sz,))

    def zrep():
        s = T.sem["zr%d_%d" % (e, c)]
        for j in range(1, 4):
            SY.dma_start(T.Z4[:, zb + 128 * j:zb + 128 * j + 128], z).then_inc(s, 16)
        return None
    add("Y", 0.3, zrep, (rz,), (("Z4", zb + 128, zb + 512),), kind="d", sem="zr%d_%d" % (e, c), val=48, lat=2.2)

    def fK(o):
        mm(o, sl("ID64"), hi, True, False)
        return mm(o, sl("ID"), lo, False, True)
    Kp = P(7)[:, 0:128]
    add("T", tt(128, 2), lambda: fK(Kp), (rhl, rs("ID64"), rs("ID")), (PR(7),))
    add("V", vt(128), lambda: V.tensor_copy(B("K16")[:, :], Kp), (PR(7),), (R("K16"),))

    def fU():
        for r in range(16):
            i = mm(P(7)[:, 128:136], T.WL[:, 128 * r:128 * r + 128], T.Z4[:, zb + r:zb + 128:16], r == 0, r == 15)
        return i
    add("T", tt(8, 16), fU, (rz, ("WL", 0, 2048)), (PR(7),))
    add("V", vt(8), lambda: V.tensor_copy(B("ua")[:, :], P(7)[:, 128:136]), (PR(7),), (R("ua"),))
    add("V", vt(8), lambda: ts(B("ub")[:, :], B("ua")[:, :], 63, None, A.bitwise_and), (R("ua"),), (R("ub"),))
    add("V", vt(8), lambda: V.tensor_tensor(B("uc")[:, :], B("ub")[:, :], B("ub")[:, :], A.mult), (R("ub"),), (R("uc"),))
    add("V", vt(8), lambda: ts(B("ud")[:, :], B("uc")[:, :], 5, 3, A.arith_shift_right, A.bitwise_and), (R("uc"),), (R("ud"),))
    add("V", vt(8), lambda: V.tensor_tensor(B("ue")[:, :], B("ud")[:, :], T.I4[:, :], A.add), (R("ud"), ("I4", 0, 8)), (R("ue"),))
    add("V", vt(8), lambda: V.tensor_copy(B("c16")[:, :], B("ue")[:, :]), (R("ue"),), (R("c16"),))
    wa, wb = 512 * c, 512 * c + 512
    add("S", vt(128, GAT), lambda: S.activation(B("Gs")[:, :], T.Gf[:, wa:wb].indirect(B("c16")[:, 0:8]), AF.Copy),
        (R("c16"), ("Gf", wa, wb)), (R("Gs"),))
    add("V", vt(128), lambda: V.tensor_tensor(B("p1")[:, :], B("Gs")[:, :], Kp, A.mult), (R("Gs"), PR(7)), (R("p1"),))

    def fv():
        mm(P(7)[:, 256:384], T.W37[:, :], z, True, False)
        return mm(P(7)[:, 256:384], T.IDF[:, :], B("Gs")[:, :], False, True)
    add("T", tt(128, 5), fv, (rz, ("W37", 0, 128), ("IDF", 0, 128), R("Gs")), (PR(7),))
    add("V", vt(128), lambda: ts(B("pr")[:, :], B("p1")[:, :], 5, None, A.arith_shift_right), (R("p1"),), (R("pr"),))
    add("V", vt(128), lambda: V.tensor_tensor(B("s1")[:, :], B("pr")[:, :], P(7)[:, 256:384], A.add), (R("pr"), PR(7)), (R("s1"),))
    add("V", vt(128), lambda: ts(B("s2")[:, :], B("s1")[:, :], 4095, None, A.bitwise_and), (R("s1"),), (R("s2"),))
    add("V", vt(128), lambda: V.tensor_copy(B("s16")[:, :], B("s2")[:, :]), (R("s2"),), (R("s16"),))
    for hf in range(4):
        def fx(hf=hf):
            return S.activation(B("x")[:, 512 * hf:512 * hf + 512], T.X[:, :].indirect(B("K16")[:, 32 * hf:32 * hf + 32]), AF.Copy)
        add("S", vt(512, GAT), fx, (R("K16"), ("X", 0, 4096)), (R("x", 512 * hf, 512 * hf + 512),))
    add("S", vt(128, GAT), lambda: S.activation(B("Wo")[:, :], T.Wf[:, wa:wb].indirect(B("c16")[:, 0:8]), AF.Copy),
        (R("c16"), ("Wf", wa, wb)), (R("Wo"),))
    add("V", vt(128), lambda: V.tensor_tensor(B("dk")[:, :], B("Wo")[:, :], Kp, A.subtract), (R("Wo"), PR(7)), (R("dk"),))
    for pc in range(4):
        a, b = 512 * pc, 512 * pc + 512
        yo = B("s16")[:, 32 * pc:32 * pc + 32]
        if pc in YS:
            bk = pc % 2

            def fy(a=a, b=b, yo=yo):
                return S.activation(B("d")[:, a:b], T.Y[:, :].indirect(yo), AF.Copy)
            add("S", vt(512, GAT), fy, (R("s16"), ("Y", 0, 4096)), (R("d", a, b),))

            def fd(a=a, b=b, bk=bk):
                mm(P(bk)[:, 0:512], sl("NID"), B("x")[:, a:b], True, False)
                return mm(P(bk)[:, 0:512], sl("ID"), B("d")[:, a:b], False, True)
            add("T", tt(512, 2), fd, (R("x", a, b), R("d", a, b), rs("ID"), rs("NID")), (PR(bk),))
            add("S", vt(512), lambda a=a, b=b, bk=bk: S.activation(B("d")[:, a:b], P(bk)[:, 0:512], AF.Abs), (PR(bk),), (R("d", a, b),))
        else:
            def fy(a=a, b=b, yo=yo):
                return V.tensor_tensor(B("d")[:, a:b], T.Y[:, :].indirect(yo), B("x")[:, a:b], A.subtract)
            add("V", vt(512, GAT), fy, (R("s16"), ("Y", 0, 4096), R("x", a, b)), (R("d", a, b),))

            def fa(a=a, b=b):
                return S.activation(B("d")[:, a:b], B("d")[:, a:b], AF.Abs)
            add("S", vt(512), fa, (R("d", a, b),), (R("d", a, b),))
        if pc % 2:
            hf = pc // 2

            def fD(hf=hf):
                a, b = 1024 * hf, 1024 * hf + 1024
                for k in range(16):
                    i = mm(P(4)[:, 64 * hf:64 * hf + 64], T.L1[:, 128 * k:128 * k + 128], B("d")[:, a + k:b:16], k == 0, k == 15)
                return i
            add("T", tt(64, 16), fD, (R("d", 1024 * hf, 1024 * hf + 1024), ("L1", 0, 2048)), (PR(4),))
    for bk in range(4):
        pb = bk % 2

        def fb(bk=bk, pb=pb):
            mm(P(pb)[:, 0:512], sl("NID"), T.Z4[:, zb:zb + 512], True, False)
            for j in range(4):
                i = mm(P(pb)[:, 128 * j:128 * j + 128], sl("ID"), B("x")[:, 4 * bk + j:2048:16], False, j == 3)
            return i
        add("T", tt(512, 2), fb, (("Z4", zb, zb + 512), R("x"), rs("ID"), rs("NID")), (PR(pb),))
        for j in range(2):
            pr = 2 * bk + j

            def fs(bk=pb, j=j, pr=pr):
                return S.activation(B("sg")[:, 256 * pr:256 * pr + 256], P(bk)[:, 256 * j:256 * j + 256], AF.Sign, bias=0.5 - 16.0 * (7 - pr))
            add("S", vt(256), fs, (PR(pb),), (R("sg", 256 * pr, 256 * pr + 256),))
    for bk in range(4):
        def fc(bk=bk):
            for j in range(4):
                k = 4 * bk + j
                i = mm(P(5)[:, 0:128], T.L1[:, 128 * k:128 * k + 128], B("sg")[:, 128 * k:128 * k + 128], k == 0, False)
            return i
        add("T", tt(128, 4), fc, (R("sg", 512 * bk, 512 * bk + 512), ("L1", 0, 2048)), (PR(5),))
    thr = 11 if first else 12
    o, f, h = B("o")[:, :], B("f")[:, :], B("h")[:, :]
    add("V", vt(128), lambda: ts(o, P(4)[:, 0:128], col(thr), 1024.0, A.is_ge, A.mult), (PR(4), rc(thr)), (R("o"),))
    add("T", tt(128), lambda: mm(P(5)[:, 0:128], sl("IDm32"), o, False, True), (R("o"), rs("IDm32")), (PR(5),))
    add("S", vt(128), lambda: S.activation(B("hd")[:, :], P(5)[:, 0:128], AF.Relu), (PR(5),), (R("hd"),))

    def fE():
        mm(P(4)[:, 128:256], sl("DE"), sl("ones"), True, False)
        return mm(P(4)[:, 128:256], sl("SD"), o, False, True)
    add("T", tt(128, 2), fE, (R("o"), rs("DE"), rs("SD"), rs("ones")), (PR(4),))
    add("V", vt(128), lambda: V.tensor_tensor(B("eo")[:, :], o, P(4)[:, 128:256], A.mult), (R("o"), PR(4)), (R("eo"),))

    def fF():
        mm(P(5)[:, 128:256], sl("TGE"), B("hd")[:, :], True, False)
        return mm(P(5)[:, 128:256], sl("IDh"), o, False, True)
    add("T", tt(128, 2), fF, (R("o"), R("hd"), rs("TGE"), rs("IDh")), (PR(5),))
    add("S", vt(128), lambda: S.activation(f, P(5)[:, 128:256], AF.Relu, bias=1.0, scale=-1.0, accum_out=B("Fs")[:, 0:1]),
        (PR(5),), (R("f"), R("Fs")))
    add("V", vt(128), lambda: V.tensor_tensor(h, P(5)[:, 128:256], o, A.is_gt), (PR(5), R("o")), (R("h"),))

    def fX():
        mm(P(4)[:, 384:512], sl("ID"), f, True, True)
        mm(P(4)[:, 256:384], sl("DX"), sl("ones"), True, False)
        mm(P(4)[:, 256:384], sl("SD"), o, False, False)
        return mm(P(4)[:, 256:384], sl("NBD"), f, False, True)
    add("T", tt(128, 4), fX, (R("o"), R("f"), rs("DX"), rs("SD"), rs("NBD"), rs("ones"), rs("ID")), (PR(4),))

    def fK2():
        return fK(P(6)[:, 256:384])
    add("T", tt(128, 2), fK2, (rhl, rs("ID64"), rs("ID")), (PR(6),))
    add("V", vt(128), lambda: V.tensor_tensor(B("dl")[:, :], B("dk")[:, :], P(4)[:, 384:512], A.mult), (R("dk"), PR(4)), (R("dl"),))
    add("V", vt(128), lambda: V.tensor_tensor(B("val")[:, :], B("dl")[:, :], P(6)[:, 256:384], A.add), (R("dl"), PR(6)), (R("val"),))
    add("S", vt(128), lambda: S.activation(B("h64")[:, :], B("val")[:, :], AF.Copy, bias=8224.5), (R("val"),), (R("h64"),))
    add("V", vt(128), lambda: V.tensor_tensor(B("m")[:, :], h, P(4)[:, 256:384], A.mult), (R("h"), PR(4)), (R("m"),))

    def fW(o_, dk, hs):
        mm(o_, sl(dk), sl("ones"), True, False)
        mm(o_, sl("NSLT"), o, False, False)
        mm(o_, sl("ID16"), B("eo")[:, :], False, False)
        return mm(o_, sl("ID64"), B("m")[:, :], False, False)
    wr_ = (R("o"), R("eo"), R("m"), rs("ones"), rs("NSLT"), rs("ID16"), rs("ID64"), rs("DK"), rs("DKL"))
    add("T", tt(128, 4), lambda: fW(P(5)[:, 256:384], "DK", None), wr_, (PR(5),))
    add("T", tt(128, 4), lambda: fW(P(4)[:, 0:128], "DKL", None), wr_, (PR(4),))
    add("T", tt(128), lambda: mm(P(5)[:, 256:384], sl("ID64t"), B("h64")[:, :], False, True), (R("h64"), rs("ID64t")), (PR(5),))
    add("T", tt(128), lambda: mm(P(4)[:, 0:128], sl("NID"), B("h64")[:, :], False, True), (R("h64"), rs("NID")), (PR(4),))
    add("V", vt(128), lambda: ts(B("WW")[:, 0:128], P(5)[:, 256:384], -129.0, None, A.add), (PR(5),), (R("WW", 0, 128),))
    add("V", vt(128), lambda: V.tensor_tensor(B("WW")[:, 128:256], B("val")[:, :], P(4)[:, 0:128], A.add), (R("val"), PR(4)), (R("WW", 128, 256),))
    if c == 1 and not last:
        def fF2():
            mm(P(6)[:, 384:385], T.ONE16[:, :], T.Fs0[:, 0:1], True, False)
            return mm(P(6)[:, 384:385], T.ONE16[:, :], T.Fs1[:, 0:1], False, True)
        add("T", tt(64, 8), fF2, (("Fs0", 0, 1), ("Fs1", 0, 1), ("ONE16", 0, 128)), (PR(6),))
        add("V", vt(1), lambda: V.tensor_copy(T.Fi[:, 0:1], P(6)[:, 384:385]), (PR(6),), (("Fi", 0, 1),))
        add("V", vt(1), lambda: ts(T.Fj[:, 0:1], T.Fi[:, 0:1], 511, None, A.bitwise_and), (("Fi", 0, 1),), (("Fj", 0, 1),))
        add("V", vt(1), lambda: V.tensor_tensor(col(12), T.Fj[:, 0:1], col(11), A.add), (("Fj", 0, 1), rc(11)), (rc(12),))
    for q in range(15):
        def fq(q=q):
            return ts(B("CL")[:, 256 * q:256 * q + 256], B("WW")[:, :], 64.0 * (q + 1), None, A.min)
        add("V", vt(256, .5), fq, (R("WW"),), (R("CL", 256 * q, 256 * q + 256),))
    add("T", tt(256), lambda: mm(P(6)[:, 0:256], T.PQ[:, 1920:2048], B("WW")[:, :], True, False), (R("WW"), ("PQ", 0, 2048)), (PR(6),))
    for q0 in range(0, 15, 3):
        def fp(q0=q0):
            for q in range(q0, q0 + 3):
                i = mm(P(6)[:, 0:256], T.PQ[:, 128 * q:128 * q + 128], B("CL")[:, 256 * q:256 * q + 256], False, q == 14)
            return i
        add("T", tt(256, 3), fp, (R("CL", 256 * q0, 256 * q0 + 768), ("PQ", 0, 2048)), (PR(6),))
    add("S", vt(256), lambda: S.activation(T.HS[:, hb:hb + 256], P(6)[:, 0:256], AF.Identity, bias=col(5)), (PR(6), rc(5)), (("HS", hb, hb + 256),))
    sh = None
    if not last:
        nb = 256 * (n + 2)

        def sendh():
            return g.remote_dma(out_ap=T.HL[:, nb:nb + 256], in_ap=T.HS[:, hb:hb + 256], remote_sem=T.sem["ah%d_%d" % (e + 1, c)],
                                local_sem=T.sem.loc, pid=pid, routing_id=rid, dma_engine_mask=emask)
        sh = add("G", 1.0, sendh, (("HS", hb, hb + 256),), (), kind="s")
    else:
        def fK3():
            mm(P(7)[:, 0:128], sl("ID64"), T.HS[:, hb:hb + 128], True, False)
            return mm(P(7)[:, 0:128], sl("ID"), T.HS[:, hb + 128:hb + 256], False, True)
        add("T", tt(128, 2), fK3, (("HS", hb, hb + 256), rs("ID64"), rs("ID")), (PR(7),))
        add("S", vt(128), lambda: S.activation(T.YK[:, 128 * c:128 * c + 128], P(7)[:, 0:128], AF.Copy), (PR(7),), (("YK", 128 * c, 128 * c + 128),))
        add("Y", .1, lambda: SY.dma_start(T.yk[:, 128 * c:128 * c + 128], T.YK[:, 128 * c:128 * c + 128]), (("YK", 128 * c, 128 * c + 128),), (),
            kind="d", sem="st%d" % c, val=16, lat=2.2)
    add("V", vt(128, SCA), lambda: V.tensor_tensor(T.Wf[:, wa:wb].indirect(B("c16")[:, 0:8]), B("Wo")[:, :], B("dl")[:, :], A.subtract),
        (R("Wo"), R("dl"), R("c16")), (("Wf", wa, wb),))
    if last:
        add("Y", .1, lambda: SY.dma_start(T.yw[:, wa:wb], T.Wf[:, wa:wb]), (("Wf", wa, wb),), (), kind="d", sem="st%d" % (2 + c), val=16, lat=2.5)
    for bk in range(4):
        pb = 2 + bk % 2

        def fm(bk=bk, pb=pb):
            for j in range(4):
                k = 4 * bk + j
                mm(P(pb)[:, 128 * j:128 * j + 128], sl("ID"), B("x")[:, k:2048:16], True, False)
                i = mm(P(pb)[:, 128 * j:128 * j + 128], T.L2[:, 128 * k:128 * k + 128], h, False, True)
            return i
        add("T", tt(128, 8), fm, (R("h"), R("x"), ("L2", 0, 2048), rs("ID")), (PR(pb),))
        for j in range(2):
            def fM(bk=bk, j=j, pb=pb):
                src = P(pb)[:, 256 * j:256 * j + 256]
                if bk == 0 and j == 0:
                    return ts(B("AC")[:, :], src, 256.0, None, A.max)
                return V.tensor_tensor(B("AC")[:, :], B("AC")[:, :], src, A.max)
            add("V", vt(256), fM, (PR(pb),) if bk == 0 and j == 0 else (R("AC"), PR(pb)), (R("AC"),))
    add("V", vt(128, 2), lambda: V.tensor_tensor(B("mz")[:, :], B("AC")[:, 0:128], B("AC")[:, 128:256], A.max), (R("AC"),), (R("mz"),))
    zs = 128 * n

    def fz():
        mm(P(2)[:, 0:128], sl("ID"), z, True, False)
        return mm(P(2)[:, 0:128], sl("NID"), B("mz")[:, :], False, True)
    add("T", tt(128, 2), fz, (rz, R("mz"), rs("ID"), rs("NID")), (PR(2),))
    add("S", vt(128), lambda: S.activation(T.ZS[:, zs:zs + 128], P(2)[:, 0:128], AF.Abs, bias=256.0), (PR(2),), (("ZS", zs, zs + 128),))
    if not last:
        nz = 512 * (n + 2)

        def sendz():
            return g.remote_dma(out_ap=T.Z4[:, nz:nz + 128], in_ap=T.ZS[:, zs:zs + 128], remote_sem=T.sem["az%d_%d" % (e + 1, c)],
                                local_sem=T.sem.loc, pid=pid, routing_id=rid, dma_engine_mask=emask)
        sz = add("G", 1.0, sendz, (("ZS", zs, zs + 128),), (), kind="s")
        _lead_sends[(e, c)] = (sh, sz)
    else:
        add("Y", .1, lambda: SY.dma_start(T.yz[:, 128 * c:128 * c + 128], T.ZS[:, zs:zs + 128]), (("ZS", zs, zs + 128),), (),
            kind="d", sem="st%d" % (4 + c), val=16, lat=2.2)


_lead_sends = {}
